import numpy as np, ml_dtypes
CORES = [3,7,11,15,131,135,139,143]
N = 8
BF = ml_dtypes.bfloat16
E, D, R, NB, M, PH, P = 3072, 192, 384, 3, 9, 2, 5
S = NB + 2 - PH % 2
def link(rng, a, b):
    k = np.arange(E); k[:D] += D; k[a] = b
    s = np.setdiff1d(np.arange(D, E), a); t = np.setdiff1d(np.concatenate([np.arange(D), np.arange(2 * D, E)]), b)
    k[s] = rng.permutation(t)
    return k
def near(rng, n):
    return link(rng, 2 * D + rng.permutation(R)[:n], rng.permutation(D)[:n])
def ways(rng, late, fresh):
    pool = 2 * D + R + rng.permutation(E - 2 * D - R); at = [0]; o = 2 * D + rng.permutation(R); tab = [([], []), ([], [])]
    def join(a, b, t):
        tab[t & 1][0].append(a); tab[t & 1][1].append(b)
    def go(a, t, n):
        for i in range(t, t + n):
            b = pool[at[0]:at[0] + len(a)]; at[0] += len(a)
            join(a, b, i); a = b
        return a
    if late:
        join(go(o[:D], 0, PH), rng.permutation(D), PH); go(o[D:], 0, PH + 1)
    else:
        w = go(o[:D], 0, PH - 1); join(w, rng.permutation(D), PH - 1)
        u = go(o[D:], 0, 2 * PH); s = go(D + np.arange(D), PH, PH)
        m = np.concatenate([u, s]); to = m
        if PH % 2 == 0:
            m = np.concatenate([m, w]); to = np.concatenate([to, o[:D]])
        if fresh: go(m, 2 * PH, 1)
        else: join(m, rng.permutation(to), 2 * PH)
    return [link(rng, np.concatenate(a), np.concatenate(b)) for a, b in tab]
def both(rng, one):
    p = [[one(r, g) for g in range(8)] for r in range(N)]
    return [np.array([[p[r][g][i] for g in range(8)] for r in range(N)]) for i in range(2)]
def some(rng):
    return both(rng, lambda r, g: (near(rng, int(rng.integers(D // 8, D // 2))), near(rng, int(rng.integers(0, D // 2)))))
def values(rng):
    e = rng.choice(np.array([0.5, 1.0, 2.0]), (N, 8, 1, E))
    x = np.minimum(np.floor(16 * rng.random((N, 8, 16, E)) ** e), 15).astype(np.int64)
    q = np.minimum(np.floor(16 * rng.random((N, 8, 16, R)) * rng.random((N, 8, 1, R))), 15).astype(np.int64)
    return x, q
def pack(k, x, q):
    return {"k0": k[0].astype(np.int32), "k1": k[1].astype(np.int32), "x": np.ascontiguousarray(x.reshape(N, 128, E)).astype(np.float32).astype(BF),
            "q": np.ascontiguousarray(q.reshape(N, 128, R)).astype(np.float32).astype(BF)}
def setup_inputs(rng):
    x, q = values(rng)
    return pack(some(rng), x, q)
def setup_inputs_full(rng):
    x, q = values(rng)
    def one(r, g):
        if r < S: return ways(rng, False, r > NB)
        if g == 6: return ways(rng, True, False)
        if g == 7: return [link(rng, D + rng.permutation(D), rng.permutation(D)) for i in range(2)]
        n = (D, D, D - 1, D, 1, D // 2)[g]
        return near(rng, n), near(rng, D // 4)
    q[:, :5] = 0
    x[:S] = rng.integers(13, 16, (S, 8, 16, E)); q[:S] = rng.integers(0, 14, (S, 8, 16, R))
    x[S:, 6] = rng.integers(13, 16, (N - S, 16, E)); q[S:, 6] = rng.integers(0, 14, (N - S, 16, R))
    return pack(both(rng, one), x, q)
def setup_inputs_ties(rng):
    hi = rng.integers(4, 16, (N, 8, 1, 1)); cnt = rng.integers(M - 1, M + 2, (N, 8, 1, E)); off = 2 * rng.integers(0, 2, (N, 8, 1, E))
    top = np.argsort(rng.random((N, 8, E, 16)), axis=-1).transpose(0, 1, 3, 2) < cnt
    x = hi - 1 + top - off; q = np.broadcast_to(hi - 2 * rng.integers(0, 2, (N, 8, 1, R)), (N, 8, 16, R))
    return pack(some(rng), x, q)
def setup_inputs_chain(rng):
    def one(r, g):
        h = D // 2
        return [link(rng, np.concatenate([2 * D + rng.permutation(R)[:h], D + rng.permutation(D)[:D - h]]), rng.permutation(D)) for i in range(2)]
    x = rng.integers(10, 16, (N, 8, 16, E)); q = rng.integers(0, 9, (N, 8, 16, R))
    return pack(both(rng, one), x, q)
def setup_inputs_ends(rng):
    x, q = values(rng)
    def one(r, g):
        a = np.arange(2 * D, E)
        if g == 2: return [link(rng, a, a) for i in range(2)]
        if g == 3:
            k = near(rng, D // 2); return k, k
        u = np.array([2 * D, 2 * D + R - 1, 2 * D + 1]); w = np.array([0, D - 1, E - 1])
        return link(rng, u, w), link(rng, u, w[::-1])
    x[:, 0] = 0; q[:, 0] = 0; x[:, 1] = 15; q[:, 1] = 15; x[:, 6] = 0; q[:, 6] = rng.integers(0, 3, (N, 1, R))
    q[..., 0] = 0; q[..., 1] = 0; q[..., R - 1] = 0
    return pack(both(rng, one), x, q)
def setup_inputs_spread(rng):
    x = np.minimum(np.floor(np.exp2(4 * rng.random((N, 8, 1, E))) * rng.random((N, 8, 16, E))), 15).astype(np.int64)
    q = np.minimum(np.floor(np.exp2(4 * rng.random((N, 8, 1, R))) * rng.random((N, 8, 16, R))), 15).astype(np.int64)
    c = np.array([0, 1, D // 2, D])
    return pack(both(rng, lambda r, g: (near(rng, int(rng.choice(c))), near(rng, int(rng.choice(c))))), x, q)
def check_inputs(d):
    bad = []
    for k in ("k0", "k1"):
        v = np.asarray(d[k]).astype(np.int64)
        if np.any(np.sort(v, axis=-1) != np.arange(E)): bad.append(k + " is no permutation")
        if np.any(v[..., :D] != D + np.arange(D)): bad.append("doors of " + k)
    for k in ("x", "q"):
        v = np.asarray(d[k]).astype(np.float64)
        if not np.all((v >= 0) & (v <= 15) & (v == np.rint(v))): bad.append("range of " + k)
    return bad
def reference(k0, k1, x, q):
    k = np.stack([k0, k1]).astype(np.int64)
    X = x.astype(np.float32).astype(np.int64).reshape(N, 8, 16, E)
    Q = np.concatenate([q.astype(np.float32).astype(np.int64).reshape(N, 8, 16, R), np.zeros((N, 8, 16, D), np.int64)], axis=3)
    first = np.concatenate([2 * D + np.arange(R), D + np.arange(D)])
    v = np.tile(first, (N, 8, 1)); b = v.copy()
    act = np.zeros((N, 8, R + D), bool); act[:, :, :R] = True
    mark = np.zeros((N, 8, E), bool); mark[:, :, 2 * D:2 * D + R] = True
    turn = np.zeros((N, 8, E), np.int64); wait = np.zeros((N, 8, R + D), bool)
    def enough(hi, lo, axis):
        return np.add.reduce((hi >= lo).astype(np.int64), axis=axis) >= M
    def retreat(m):
        Q[:] = Q - m[:, :, None, :].astype(np.int64)
        n, g, w = np.nonzero(m & (b != v))
        p = b[n, g, w]; o = v[n, g, w]; h = turn[n, g, p]; back = k[h, n, g, p]
        xo = X[n, g, :, o]; xp = X[n, g, :, p]
        k[h, n, g, p] = np.where(enough(xo, xp, 1), o, p)
        X[n, g, :, p] = np.maximum(xp, xo - 1)
        b[n, g, w] = back; v[n, g, w] = p
    for t in range(PH * P):
        f = t & 1
        go = act & (v >= D)
        c = np.take_along_axis(k[f], v, 2)
        ok = go & ~np.take_along_axis(mark, c, 2) & enough(np.take_along_axis(X, c[:, :, None, :], 3), Q, 2)
        n, g, w = np.nonzero(ok); o = v[n, g, w]; to = c[n, g, w]
        k[f, n, g, o] = b[n, g, w]; turn[n, g, o] = f; mark[n, g, to] = True
        Q[n, g, :, w] = np.maximum(Q[n, g, :, w], X[n, g, :, to]) - 2
        b[n, g, w] = o; v[n, g, w] = to
        retreat(go & ~ok)
        if t % PH == PH - 1:
            on = act & (v < D); stay = on & wait; new = on & ~wait
            n, g, w = np.nonzero(new); j = v[n, g, w]; to = (n + 1 + j // (D // NB)) % N
            Q[to, g, :, R + j] = Q[n, g, :, w]; act[to, g, R + j] = True; mark[to, g, D + j] = True
            n, g, w = np.nonzero(stay); j = v[n, g, w]; to = (n + 1 + j // (D // NB)) % N
            X[n, g, :, j] = X[to, g, :, D + j]
            retreat(stay)
            wait = new
    return {"yk0": k[0].astype(np.float32), "yk1": k[1].astype(np.float32), "yx": X.reshape(N, 128, E).astype(np.float32).astype(BF)}

@@ -1,0 +1,507 @@
+from concourse.bass import DstId, RemoteDMATransfer
+from concourse.mybir import AluOpType as A, ActivationFunctionType as F
+
+E, ND, NR, NW, M = 3072, 192, 384, 576, 36
+LOWB, TB, XB, QB, WEND = 192, 784, 3856, 6928, 7504
+OB = TB - LOWB
+LW = 8192 + 768
+CW = (E - ND) // 16
+MAGIC = 12582912.0
+
+
+def sb(n, dtype="float32"):
+    return ("sbuf", [128, n], dtype)
+
+
+SCRATCH = {
+    "W": sb(WEND, "bfloat16"), "WQ": sb(TB + E, "bfloat16"), "KT": sb(E, "bfloat16"), "L": sb(LW), "IOT": sb(E),
+    "ST": sb(2048, "bfloat16"), "ID": sb(256, "bfloat16"), "BD": sb(256, "bfloat16"), "idf": sb(128), "bdf": sb(128),
+    "kc": sb(384, "int32"), "klo": sb(384, "int32"), "kp": sb(768, "bfloat16"), "kz": sb(768, "bfloat16"),
+    "kf": sb(384), "kd": sb(ND), "cc": sb(384), "pi": sb(8, "int32"), "pf": sb(8), "g8": sb(8), "b8": sb(8, "bfloat16"),
+    "jraw": sb(M), "jj": sb(M), "qsj": sb(M),
+    "D": sb(NW, "bfloat16"), "cmp": sb(NW, "bfloat16"), "G": sb(NW, "bfloat16"), "Xn": sb(NW, "bfloat16"),
+    "Kg": sb(NW, "bfloat16"), "cmpb": sb(NW, "bfloat16"), "Y": sb(NW, "bfloat16"), "Y0": sb(NW, "bfloat16"),
+    "m1": sb(NW, "bfloat16"), "lw": sb(NW), "xd": sb(ND, "bfloat16"),
+    "gt": sb(ND, "bfloat16"), "gb": sb(ND, "bfloat16"), "gbm": sb(ND, "bfloat16"), "gb1": sb(ND, "bfloat16"),
+    "snd": sb(4 * ND, "bfloat16"), "rf": sb(4 * ND, "bfloat16"),
+    "NEW0": sb(108), "NEW1": sb(108), "U0": sb(108, "uint16"), "U1": sb(108, "uint16"),
+    "cu": sb(M, "uint16"), "lo0": sb(M, "uint16"), "lo1": sb(M, "uint16"), "lv": sb(M, "uint16"),
+    "AA0": sb(108), "AA1": sb(108), "DF": sb(108), "MM": sb(108),
+    "Z0": sb(8 * M, "int32"), "Z1": sb(8 * M, "int32"), "zm": sb(6 * M), "zb": sb(6 * M),
+    "bid0": sb(M, "int32"), "bid1": sb(M, "int32"), "dv0": sb(M), "dv1": sb(M),
+    "st0": sb(M, "bfloat16"), "st1": sb(M, "bfloat16"), "adv": sb(M, "bfloat16"),
+    "s0": sb(M), "s1": sb(M), "s2": sb(M), "s3": sb(M), "s5": sb(M), "s6": sb(M), "s7": sb(M), "s8": sb(M),
+    "s9": sb(M), "sa": sb(M), "om": sb(E, "bfloat16"), "oy": sb(E, "bfloat16"),
+    "pcnt": ("psum", [128, 512], "float32"), "pk": ("psum", [128, 512], "float32"),
+    "pe": ("psum", [128, 1024], "float32"), "pcb": ("psum", [128, 512], "float32"),
+    "pav": ("psum", [128, 512], "float32"), "pst": ("psum", [128, 512], "float32"),
+    "pv": ("psum", [128, 512], "float32"),
+}
+NDMA = 25
+SEMAPHORES = (["cv", "cs", "cp", "cg"] + ["d%d" % i for i in range(NDMA)] + ["fa%d" % i for i in range(4)]
+              + ["ba%d" % i for i in range(4)] + ["fl%d" % i for i in range(4)] + ["bl%d" % i for i in range(4)])
+XCH = 4
+
+
+def pow2(n):
+    k = 1
+    while 2 * k <= n:
+        k *= 2
+    return k
+
+
+def engine_plan(topo, src, dsts):
+    lists = [topo.engines(src, d) for d in dsts]
+    few = min(len(e) for e in lists)
+    tight = [i for i in range(len(dsts)) if len(lists[i]) == few]
+    masks = [0] * len(dsts)
+    pool = list(lists[tight[0]])
+    used = 0
+    for n, i in enumerate(tight):
+        k = pow2(len(pool) // (len(tight) - n))
+        for e in pool[:k]:
+            masks[i] |= 1 << e
+        pool = pool[k:]
+        used |= masks[i]
+    for i in range(len(dsts)):
+        if i not in tight:
+            free = [e for e in lists[i] if not used >> e & 1]
+            for e in free[:pow2(len(free))]:
+                masks[i] |= 1 << e
+            used |= masks[i]
+    return masks
+
+
+def bits(m):
+    return bin(m).count("1")
+
+
+def rank_program(g, core, T, topo):
+    rank = T.rank_of(core)
+    if rank is None:
+        return
+    N = len(T.cores)
+    Q = {"v": g.vector, "s": g.scalar, "p": g.tensor, "g": g, "y": g.sync}
+    csem = {"v": "cv", "s": "cs", "p": "cp", "g": "cg"}
+    count = {"v": 0, "s": 0, "p": 0, "g": 0}
+    waited = {q: {} for q in Q}
+    log = {}
+    total = {}
+    nd = [0]
+
+    def wait(q, sem, val):
+        if waited[q].get(sem, 0) < val:
+            Q[q].wait_ge(T.sem[sem], val)
+            waited[q][sem] = val
+
+    def order(q, reads, writes):
+        need = {}
+        for kind, regs in ((0, reads), (1, writes)):
+            for b, lo, hi in regs:
+                psum = b in SCRATCH and SCRATCH[b][0] == "psum"
+                for l2, h2, w2, sem, val in log.get(b, []):
+                    if psum and sem != csem[q]:
+                        if l2 // 512 > (hi - 1) // 512 or (h2 - 1) // 512 < lo // 512:
+                            continue
+                    elif l2 >= hi or h2 <= lo or not (kind or w2):
+                        continue
+                    need[sem] = max(need.get(sem, 0), val)
+        for sem in need:
+            wait(q, sem, need[sem])
+
+    def note(reads, writes, sem, val):
+        total[sem] = max(total.get(sem, 0), val)
+        for b, lo, hi in writes:
+            log[b] = [x for x in log.get(b, []) if not (x[0] >= lo and x[1] <= hi)] + [[lo, hi, 1, sem, val]]
+        for b, lo, hi in reads:
+            log.setdefault(b, []).append([lo, hi, 0, sem, val])
+
+    def op(q, fn, reads, writes):
+        order(q, reads, writes)
+        ins = fn(Q[q])
+        count[q] += 1
+        ins.then_inc(T.sem[csem[q]], 1)
+        note(reads, writes, csem[q], count[q])
+
+    def dma(q, out, in_, reads, writes):
+        order(q, reads, writes)
+        sem = "d%d" % nd[0]
+        nd[0] += 1
+        Q[q].dma_start(out, in_).then_inc(T.sem[sem], 16)
+        note(reads, writes, sem, 16)
+
+    def r(b, lo=0, hi=M):
+        return (b, lo, hi)
+
+    def ap(x):
+        return T[x[0]][:, x[1]:x[2]]
+
+    def ts(out, in0, s1, s2, o0, o1=None, extra=()):
+        if o1 is None:
+            op("v", lambda e: e.tensor_scalar(ap(out), ap(in0), s1, None, o0), [in0] + list(extra), [out])
+        else:
+            op("v", lambda e: e.tensor_scalar(ap(out), ap(in0), s1, s2, o0, o1), [in0] + list(extra), [out])
+
+    def tt(out, a, b, o):
+        op("v", lambda e: e.tensor_tensor(ap(out), ap(a), ap(b), o), [a, b], [out])
+
+    def cp(out, a):
+        op("v", lambda e: e.tensor_copy(ap(out), ap(a)), [a], [out])
+
+    def ms(out, c):
+        op("v", lambda e: e.memset(ap(out), c), [], [out])
+
+    def ind(win, off):
+        return ap(win).indirect(ap(off))
+
+    def ttg(out, win, off, b, o):
+        op("v", lambda e: e.tensor_tensor(ap(out), ind(win, off), ap(b), o), [win, off, b], [out])
+
+    def act(out, a, func, bias=0.0, scale=1.0, also=()):
+        op("s", lambda e: e.activation(ap(out), ap(a), func, bias=bias, scale=scale), [a], [out] + list(also))
+
+    def actg(out, win, off, bias=0.0):
+        op("s", lambda e: e.activation(ap(out), ind(win, off), F.Identity, bias=bias), [win, off], [out])
+
+    def iota(out, pattern, base, cm):
+        op("g", lambda e: e.iota(ap(out), pattern, base, cm, allow_small_or_imprecise_dtypes=True), [], [out])
+
+    def fill(out, c):
+        iota(out, [[0, out[2] - out[1]]], c, 0)
+
+    def mm(groups):
+        def fn(e):
+            for out, terms in groups:
+                for k, (a, b) in enumerate(terms):
+                    ins = e.matmul(ap(out), ap(a), ap(b), k == 0, k == len(terms) - 1)
+            return ins
+        op("p", fn, [x for out, terms in groups for ab in terms for x in ab], [out for out, terms in groups])
+
+    def wrap(ps, src, n):
+        def fn(e):
+            for i in range(16):
+                ins = e.matmul(T[ps][:, 0:n // 16], T.ST[:, 128 * i:128 * i + 128], T[src][:, i:n:16], i == 0, i == 15)
+            return ins
+        op("p", fn, [r("ST", 0, 2048), r(src, 0, n)], [r(ps, 0, n // 16)])
+
+    def exchange(sign, src_buf, src_lo, land, land_lo, asem, lsem):
+        dsts = [T.cores[(rank + sign * (1 + h)) % N] for h in range(3)]
+        masks = engine_plan(topo, core, dsts)
+        order("g", [r(src_buf, src_lo, src_lo + ND)], [])
+        trs = []
+        for h in range(3):
+            rid, pid = topo.addr(dsts[h], core)
+            trs.append(RemoteDMATransfer(dst_ids=[DstId(rid=rid, pnc=pid)], dma_engine_mask=masks[h], remote_sem=T.sem[asem],
+                                         src=T[src_buf][:, src_lo + 64 * h:src_lo + 64 * h + 64],
+                                         dst=T[land][:, land_lo + 64 * h:land_lo + 64 * h + 64]))
+        g.remote_dma_fused(trs, local_sem=T.sem[lsem])
+        note([r(src_buf, src_lo, src_lo + ND)], [], lsem, sum(bits(x) for x in masks))
+        arrive = 0
+        for h in range(3):
+            s = (rank - sign * (1 + h)) % N
+            sd = [T.cores[(s + sign * (1 + k)) % N] for k in range(3)]
+            arrive += bits(engine_plan(topo, T.cores[s], sd)[h])
+        note([], [r(land, land_lo, land_lo + ND)], asem, arrive)
+
+    Tt = r("W", TB, TB + E)
+    doors = r("W", TB, TB + ND)
+    gate0 = r("W", XB + ND, XB + 2 * ND)
+    eye, neg = r("ID", 0, 128), r("ID", 128, 256)
+    fneg, tmpd = r("pv", 128, 320), r("pv", 320, 512)
+
+    dma("y", T.kc[:, 0:192], T.k0[:], [], [r("kc", 0, 192)])
+    dma("s", T.W[:, QB:QB + NR], T.q[:], [], [r("W", QB, QB + NR)])
+    cw = E // XCH
+    for c in range(XCH):
+        dma("y" if c % 2 == 0 else "s", T.W[:, TB + c * cw:TB + (c + 1) * cw], T.x[:, c * cw:(c + 1) * cw], [],
+            [r("W", TB + c * cw, TB + (c + 1) * cw)])
+    dma("y", T.kc[:, 192:384], T.k1[:], [], [r("kc", 192, 384)])
+    op("g", lambda e: e.iota(T.pi[:, 0:1], [[1, 1]], 0, 1), [], [r("pi", 0, 1)])
+    iota(r("g8", 0, 8), [[16, 8]], 0, 0)
+    iota(r("jraw"), [[16, M]], 0, 1)
+    iota(r("idf", 0, 128), [[1, 128]], 0, -1)
+    fill(r("W", XB, XB + ND), -230)
+    fill(r("WQ", TB, TB + ND), 2)
+    fill(r("WQ", LOWB + NR, TB), 1)
+    fill(r("WQ", 0, ND), 1)
+    fill(r("W", LOWB, TB), -240)
+    fill(r("W", QB + NR, WEND), -132)
+    iota(r("IOT", 0, E), [[1, E]], 64, 0)
+    iota(r("bdf", 0, 128), [[16, 8], [0, 16]], 0, 0)
+    fill(r("m1", 0, NW), -1)
+
+    ms(r("KT", 0, 1024), 0.0)
+    ms(r("ST", 0, 2048), 0.0)
+    act(r("KT", 1024, 2048), r("KT", 0, 1024), F.Copy)
+    act(r("KT", 2048, E), r("KT", 0, 1024), F.Copy)
+    for c in range(3):
+        act(r("WQ", TB + ND + 960 * c, TB + ND + 960 * c + 960), r("KT", 0, 960), F.Identity, bias=1.0,
+            also=[r("KTz", c, c + 1)])
+    ts(r("pi", 1, 2), r("pi", 0, 1), 112, None, A.bitwise_and)
+    ts(r("pi", 2, 3), r("pi", 0, 1), 14, None, A.bitwise_and)
+    ts(r("pi", 3, 4), r("pi", 0, 1), 15, None, A.bitwise_and)
+    cp(r("pf", 0, 3), r("pi", 1, 4))
+    ts(r("b8", 0, 8), r("g8", 0, 8), T.pf[:, 0:1], None, A.is_equal, extra=[r("pf", 0, 1)])
+    ts(r("pf", 6, 7), r("pf", 2, 3), 2.0, None, A.is_equal)
+    ts(r("pf", 7, 8), r("pf", 2, 3), 3.0, None, A.is_equal)
+    for i in range(16):
+        op("v", lambda e: e.tensor_copy(T.ST[:, 129 * i:128 * i + 128:16], T.b8[:, :]), [r("b8", 0, 8)],
+           [r("ST", 128 * i, 128 * i + 128)])
+    ts(r("klo", 0, 192), r("kc", 0, 192), 63, None, A.bitwise_and)
+    ts(r("jj"), r("jraw"), T.pf[:, 0:1], None, A.subtract, extra=[r("pf", 0, 1)])
+    cp(r("kp", 0, 192), r("klo", 0, 192))
+    tt(r("kp", 384, 576), r("kc", 0, 192), r("klo", 0, 192), A.subtract)
+    for n, (lo, col) in enumerate(((0, 6), (0, 7), (384, 6), (384, 7))):
+        ts(r("kz", 192 * n, 192 * n + 192), r("kp", lo, lo + 192), T.pf[:, col:col + 1], None, A.mult, extra=[r("pf", 6, 8)])
+    wrap("pk", "kz", 768)
+    ts(r("W", XB + ND, XB + 768), r("W", TB + ND, TB + 768), -128.0, None, A.add)
+    ts(r("klo", 192, 384), r("kc", 192, 384), 63, None, A.bitwise_and)
+    ts(r("W", QB, QB + NR), r("W", QB, QB + NR), -192.0, None, A.add)
+    cp(r("W", TB + ND, TB + 768), r("W", XB + ND, XB + 768))
+    cp(r("kp", 192, 384), r("klo", 192, 384))
+    cp(r("AA0", 0, 24), r("pk", 0, 24))
+    tt(r("kp", 576, 768), r("kc", 192, 384), r("klo", 192, 384), A.subtract)
+    tt(r("AA0", 0, 24), r("AA0", 0, 24), r("pk", 24, 48), A.add)
+    ts(r("NEW1", 0, 24), r("jj", 0, 24), 384.0, None, A.add)
+    cp(r("cu", 0, 24), r("AA0", 0, 24))
+    for row, lo in ((2, 192), (3, 576), (0, 0), (1, 384)):
+        dma("y", T.KT[row:128:16, :], T.kp[:, lo:lo + 192], [r("kp", lo, lo + 192), r("KT", 0, E), r("KTz", 0, 3)],
+            [r("KTr", row, row + 1)])
+    for c in range(1, XCH):
+        act(r("W", XB + c * cw, XB + (c + 1) * cw), r("W", TB + c * cw, TB + (c + 1) * cw), F.Identity, bias=-128.0)
+
+    def setup_lists():
+        act(r("xd", 0, ND), doors, F.Identity, bias=-128.0)
+        ts(r("NEW1", 24, M), r("jj", 24, M), -192.0, None, A.add)
+        ts(eye, r("idf", 0, 128), 0.0, None, A.is_equal)
+        ms(r("AA0", 24, M), 0.0)
+        ms(r("adv"), 0.0)
+        ts(r("Z0", 2 * M, 3 * M), r("NEW1"), 8192.0, None, A.add)
+        ts(r("Z0", 3 * M, 4 * M), r("NEW1"), 8192.0, None, A.add)
+        cp(r("AA0", 72, 108), r("jj"))
+        ts(r("qsj"), r("jj"), float(QB - TB), None, A.add)
+        ts(neg, r("idf", 0, 128), 0.0, -1.0, A.is_equal, A.mult)
+        ts(r("pf", 4, 5), r("pf", 1, 2), 0.0, None, A.is_equal)
+        ts(r("pf", 5, 6), r("pf", 1, 2), 2.0, None, A.is_equal)
+
+    def setup_links():
+        mm([(r("pe", 0, 384), [(eye, r("kp", 0, 384)), (eye, r("kp", 384, 768))])])
+        act(r("kf", 0, 384), r("pe", 0, 384), F.Identity, bias=64.0)
+        dma("y", T.L[0:128:16, 0:E], T.kf[:, 0:192], [r("kf", 0, 192)], [r("L", 0, E)])
+        dma("y", T.L[0:128:16, 4096:4096 + E], T.kf[:, 192:384], [r("kf", 192, 384)], [r("L", 4096, 4096 + E)])
+
+    def setup_guests():
+        actg(r("gt", 0, ND), r("W", XB, XB + E), r("cu", 24, M), bias=-1.0)
+        for b in (3, 4, 5, 6):
+            cp(r("Z1", b * M, b * M + M), r("Z0", 3 * M, 4 * M))
+        ts(r("AA1", 72, 108), r("jj"), float(LOWB), None, A.add)
+        cp(r("Z0", 4 * M, 8 * M), r("Z1", 3 * M, 7 * M))
+        ts(r("BD", 0, 128), r("bdf", 0, 128), T.pf[:, 0:1], 300.0, A.is_equal, A.mult, extra=[r("pf", 0, 1)])
+        ts(r("BD", 128, 256), r("bdf", 0, 128), T.pf[:, 0:1], -150.0, A.is_equal, A.mult, extra=[r("pf", 0, 1)])
+        cp(r("kd", 0, ND), r("kc", 0, ND))
+        dma("y", T.yk0[:, 0:ND], T.kd[0:128:16, :], [r("kd", 0, ND)], [])
+        dma("y", T.yk1[:, 0:ND], T.kd[0:128:16, :], [r("kd", 0, ND)], [])
+        tt(r("gb", 0, ND), r("gt", 0, ND), gate0, A.max)
+        ts(r("gbm", 0, ND), r("gb", 0, ND), -150.0, None, A.add)
+
+    def kgather(t, ub):
+        f = t & 1
+        op("s", lambda e: e.activation(T.Kg[:, :], ind(r("KT", 0, E), r(ub)), F.Copy, scale=T.pf[:, 4 + f:5 + f]),
+           [r("KT", 0, E), r(ub), r("pf", 4, 6), r("KTr", 0, 4)], [r("Kg", 0, NW)])
+        wrap("pk", "Kg", NW)
+
+    def links(t):
+        bid, dv = "bid%d" % (t & 1), "dv%d" % (t & 1)
+        n = NR if t < 2 else NW
+        m = n // 16
+        if t == 0:
+            cp(r("lv"), r(bid))
+        else:
+            ts(r("s6", 0, m), r("pcb", 0, m), 9.0 if t == 9 else 1.0, None, A.is_ge)
+            tt(r("s7", 0, m), r("s6", 0, m), r(dv, 0, m), A.mult)
+            tt(r("s8", 0, m), r("s7", 0, m), r(bid, 0, m), A.add)
+            cp(r("lv", 0, m), r("s8", 0, m))
+        actg(r("lw", 0, n), r("IOT", 0, E), r("lv", 0, m))
+        lo = r("lo%d" % (t & 1), 0, m)
+        op("s", lambda e: e.activation(ind(r("L", 0, LW), lo), T.lw[:, 0:n], F.Silu), [lo, r("lw", 0, n)], [r("L", 0, LW)])
+
+    def depth(t):
+        return min(t + 1, 9 - t) + 1
+
+    def stack(t):
+        f = t & 1
+        zo, zn, zw, v = "Z%d" % f, "Z%d" % (1 - f), M * depth(t), r("NEW%d" % (1 - f))
+        ts(r(zo), v, float(4096 * f), None, A.add)
+        ts(r(zo, M, 2 * M), v, float(4096 * f), None, A.add)
+        tt(r("zm", 0, zw), r(zo, 2 * M, 2 * M + zw), r("pav", 256, 256 + zw), A.mult)
+        tt(r("pav", 0, zw), r(zo, 0, zw), r("pav", 0, zw), A.mult)
+        if t > 0:
+            tt(r("zb", 0, zw), r(zo, M, M + zw), r("pst", 0, zw), A.mult)
+            tt(r("pav", 0, zw), r("zm", 0, zw), r("pav", 0, zw), A.add)
+            tt(r(zn, M, M + zw), r("zb", 0, zw), r("pav", 0, zw), A.add)
+        else:
+            tt(r(zn, M, M + zw), r("zm", 0, zw), r("pav", 0, zw), A.add)
+        cp(r("lo%d" % f), r(zn, M, 2 * M))
+
+    for t in range(10):
+        f, ph = t & 1, t // 2
+        n = NR if t < 2 else NW
+        m = n // 16
+        thr = float(192 - 2 * t)
+        back = f == 1 and t >= 3
+        start = f == 0 and t >= 2
+        dq = f == 1 and t < 9
+        old, new, un = "NEW%d" % (1 - f), "NEW%d" % f, "U%d" % f
+        bid, dv, st = "bid%d" % f, "dv%d" % f, "st%d" % f
+        AA = "AA1" if back else "AA0"
+        v = r(old)
+        k = depth(t)
+
+        if t > 0:
+            cp(r("cu"), r("pk"))
+        if start:
+            ttg(r("D", 0, NR), Tt, r("cu", 0, 24), r("W", QB, QB + NR), A.subtract)
+            ts(fneg, doors, -140.0, -300.0, A.is_ge, A.mult)
+            if t == 2:
+                setup_guests()
+            if t == 8:
+                cp(r("W", XB, XB + ND), r("xd", 0, ND))
+            stack(t - 1)
+            act(r("cmp", 0, NR), r("D", 0, NR), F.Sign, bias=0.5 - thr)
+            tt(r("W", QB + NR, WEND), r("W", QB + NR, WEND), r("rf", ND * (ph - 1), ND * ph), A.min)
+            ttg(r("D", NR, NW), Tt, r("cu", 24, M), r("W", QB + NR, WEND), A.subtract)
+            ts(r("cmp", NR, n), r("D", NR, n), thr, 0.5, A.is_ge, A.subtract)
+        else:
+            ttg(r("D", 0, n), Tt, r("cu", 0, m), r("W", QB, QB + n), A.subtract)
+            if t == 0:
+                ts(r("cmp", 0, n), r("D", 0, n), thr, 0.5, A.is_ge, A.subtract)
+            else:
+                act(r("cmp", 0, n), r("D", 0, n), F.Sign, bias=0.5 - thr)
+        if back:
+            mm([(r("pe", 0, ND), [(eye, r("gb1", 0, ND)), (r("BD", 128, 256), r("cmp", NR, NW))])])
+        wrap("pcnt", "cmp", n)
+        if t < 9:
+            act(r("WQ", LOWB, LOWB + n), r("D", 0, n), F.Relu, bias=-thr)
+        if t >= 2:
+            wrap("pcb", "cmpb", NR if t - 1 < 2 else NW)
+        if t == 0:
+            setup_lists()
+        elif not start:
+            stack(t - 1)
+        if back:
+            tt(r("pe", 0, ND), r("gb1", 0, ND), r("pe", 0, ND), A.min)
+            tt(r("snd", ND * (ph - 1), ND * ph), gate0, r("pe", 0, ND), A.max)
+            exchange(-1, "snd", ND * (ph - 1), "W", 0, "ba%d" % (ph - 1), "bl%d" % (ph - 1))
+        if t > 0:
+            cp(r(AA), r("pk"))
+        ts(r(bid), r("Z%d" % f, 2 * M, 3 * M), 4095, None, A.bitwise_and)
+        if f == 0:
+            ts(r(st), v, 192.0, None, A.is_lt)
+        else:
+            ts(r("s0"), v, 192.0, None, A.is_lt)
+        if dq:
+            ts(r("s2"), r(AA), 192.0, None, A.is_lt)
+        if f == 1:
+            tt(r(st), r("s0"), r("st0"), A.subtract)
+        tt(r(dv), v, r(bid), A.subtract)
+        if back:
+            ts(r("s9"), r("st0"), -float(TB), float(TB), A.mult, A.add)
+        else:
+            ts(r("pv", 72, 108), v, float(OB), None, A.add)
+        if dq:
+            ts(r("s3"), r(AA), float(E), None, A.add)
+            tt(r("sa"), r("s2"), r("qsj"), A.mult)
+            tt(r("s5"), r(st), r("qsj"), A.mult)
+        else:
+            ts(r(AA, M, 72), r(AA), float(E), None, A.add)
+        tt(r("s1"), r(st), r(dv), A.mult)
+        if back:
+            tt(r("pv", 72, 108), r("s9"), v, A.add)
+        if dq:
+            tt(r(AA, M, 72), r("sa"), r("s3"), A.max)
+            tt(r("pv", M, 72), r("s5"), r(bid), A.max)
+        else:
+            tt(r("pv", M, 72), r("s1"), r(bid), A.add)
+        tt(r("pv"), r("s1"), r(bid), A.add)
+        tt(r("DF", 0, 108), r(AA, 0, 108), r("pv", 0, 108), A.subtract)
+        ts(r("adv", 0, m), r("pcnt", 0, m), 0.75, None, A.is_ge)
+        for j in range(3):
+            tt(r("MM", M * j, M * j + M), r("DF", M * j, M * j + M), r("adv"), A.mult)
+        tt(r(new, 0, 108), r("MM", 0, 108), r("pv", 0, 108), A.add)
+        cp(r(un, 0, 108), r(new, 0, 108))
+        if start:
+            mm([(r("pcnt", 0, ND), [(eye, r("gbm", 0, ND)), (r("BD", 0, 128), r("cmp", NR, NW))])])
+        mm([(r("pav", M * j, M * j + M), [(eye, r("adv"))]) for j in range(k)]
+           + [(r("pav", 256 + M * j, 256 + M * j + M), [(eye, r("WQ")), (neg, r("adv")), (neg, r(st))]) for j in range(k)])
+        if t > 0:
+            mm([(r("pst", M * j, M * j + M), [(eye, r(st))]) for j in range(k)])
+        vl, off1, o_list = r(un, 0, m), r(un, M, M + m), r(un, 72, 72 + m)
+        w0 = 0 if back else LOWB
+        wold = r("W", w0, TB + E)
+        wnew = r("W", TB, WEND if dq else QB)
+        if back:
+            if t < 9:
+                kgather(t + 1, un)
+        elif t > 0:
+            actg(r("G", 0, n), wold, o_list, bias=-1.0)
+        if t < 9:
+            ttg(r("W", QB, QB + n), r("WQ", w0, TB + E), o_list, r("W", QB, QB + n), A.add)
+        if back:
+            if t == 9:
+                actg(r("Y0", 0, n), wnew, off1)
+            actg(r("Y", 0, n), wnew, off1, bias=1.0)
+            if t < 9:
+                actg(r("G", 0, n), wold, o_list, bias=-1.0)
+        else:
+            kgather(t + 1, un)
+        if t >= 1:
+            links(t - 1)
+        if start:
+            tt(r("gb1", 0, ND), r("gb", 0, ND), r("pcnt", 0, ND), A.min)
+        if back:
+            if t == 9:
+                stack(9)
+            tt(tmpd, r("W", 0, ND), fneg, A.add)
+            if t == 9:
+                ttg(r("cmpb", 0, n), wold, o_list, r("Y0", 0, n), A.is_ge)
+                wrap("pcb", "cmpb", NW)
+            ttg(r("Xn", 0, n), wold, o_list, r("Y", 0, n), A.max)
+            tt(doors, doors, tmpd, A.max)
+            if t == 9:
+                links(9)
+            op("v", lambda e: e.tensor_tensor(ind(Tt, vl), T.Xn[:, 0:n], T.m1[:, 0:n], A.add),
+               [vl, r("Xn", 0, n), r("m1", 0, n)], [Tt])
+        else:
+            if t == 0:
+                op("v", lambda e: e.tensor_copy(T.Xn[:, 0:n], ind(wnew, off1)), [wnew, off1], [r("Xn", 0, n)])
+            else:
+                ttg(r("Xn", 0, n), wnew, off1, r("G", 0, n), A.max)
+            op("v", lambda e: e.tensor_copy(ind(Tt, vl), T.Xn[:, 0:n]), [vl, r("Xn", 0, n)], [Tt])
+        if dq:
+            exchange(1, "W", TB, "rf", ND * ph, "fa%d" % ph, "fl%d" % ph)
+        if 1 <= t < 9:
+            mm([(r("pe", lo, hi), [(eye, r("Xn", lo, hi)), (neg, r("G", lo, hi))])
+                for lo, hi in ((0, min(n, 512)), (512, n)) if hi > lo])
+            act(r("cmpb", 0, n), r("pe", 0, n), F.Sign, bias=2.5 if back else 1.5, scale=-1.0)
+        if t == 0:
+            setup_links()
+
+    dma("s", T.cc[:, 0:CW], T.L[0:128:16, ND:E], [r("L", 0, E)], [r("cc", 0, CW)])
+    dma("s", T.cc[:, CW:2 * CW], T.L[0:128:16, 4096 + ND:4096 + E], [r("L", 4096, 4096 + E)], [r("cc", CW, 2 * CW)])
+    banks = [("pcnt", 0), ("pe", 0), ("pk", 0), ("pe", 512), ("pav", 0), ("pst", 0)]
+    for c, (ps, p0) in enumerate(banks):
+        lo, hi = 512 * c, 512 * c + 512
+        src, bank = r("W", TB + lo, TB + hi), r(ps, p0, p0 + 512)
+        if c % 2 == 0:
+            mm([(bank, [(eye, src)])])
+            ts(r("om", lo, hi + 512), r("W", TB + lo, TB + hi + 512), 0.0, 128.0, A.is_lt, A.mult)
+            tt(r("oy", lo, hi), r("om", lo, hi), bank, A.add)
+        else:
+            mm([(bank, [(eye, src), (eye, r("om", lo, hi))])])
+            act(r("oy", lo, hi), bank, F.Copy)
+        dma("y" if c % 2 == 0 else "s", T.yx[:, lo:hi], T.oy[:, lo:hi], [r("oy", lo, hi)], [])
+    ts(r("kf", 0, 2 * CW), r("cc", 0, 2 * CW), MAGIC, MAGIC + 64.0, A.add, A.subtract)
+    dma("y", T.yk0[:, ND:E], T.kf[:, 0:CW], [r("kf", 0, CW)], [])
+    dma("s", T.yk1[:, ND:E], T.kf[:, CW:2 * CW], [r("kf", CW, 2 * CW)], [])
+    for sem in total:
+        wait("y", sem, total[sem])

@@ -2,42 +2,53 @@ from concourse.bass import DstId, RemoteDMATransfer
 from concourse.mybir import AluOpType as A, ActivationFunctionType as F
 
 E, ND, NR, NW, M = 3072, 192, 384, 576, 36
-LOWB, TB, XB, QB, WEND = 192, 784, 3856, 6928, 7504
-OB = TB - LOWB
-LW = 8192 + 768
+O = 64
+GAP = 4096
+TV, WEND = GAP + O, GAP + O + E
+TURN = 8192
+LW = 2 * TURN + GAP + O + 2 * ND + NR
+QB = O + E
+BIG, B = 65536.0, 32768.0
 CW = (E - ND) // 16
-MAGIC = 12582912.0
+FOLD = False
+EVEN_ON_SCALAR = False
 
 
 def sb(n, dtype="float32"):
     return ("sbuf", [128, n], dtype)
 
 
+def bf(n):
+    return sb(n, "bfloat16")
+
+
+def i32(n):
+    return sb(n, "int32")
+
+
+def u16(n):
+    return sb(n, "uint16")
+
+
 SCRATCH = {
-    "W": sb(WEND, "bfloat16"), "WQ": sb(TB + E, "bfloat16"), "KT": sb(E, "bfloat16"), "L": sb(LW), "IOT": sb(E),
-    "ST": sb(2048, "bfloat16"), "ID": sb(256, "bfloat16"), "BD": sb(256, "bfloat16"), "idf": sb(128), "bdf": sb(128),
-    "kc": sb(384, "int32"), "klo": sb(384, "int32"), "kp": sb(768, "bfloat16"), "kz": sb(768, "bfloat16"),
-    "kf": sb(384), "kd": sb(ND), "cc": sb(384), "pi": sb(8, "int32"), "pf": sb(8), "g8": sb(8), "b8": sb(8, "bfloat16"),
-    "jraw": sb(M), "jj": sb(M), "qsj": sb(M),
-    "D": sb(NW, "bfloat16"), "cmp": sb(NW, "bfloat16"), "G": sb(NW, "bfloat16"), "Xn": sb(NW, "bfloat16"),
-    "Kg": sb(NW, "bfloat16"), "cmpb": sb(NW, "bfloat16"), "Y": sb(NW, "bfloat16"), "Y0": sb(NW, "bfloat16"),
-    "m1": sb(NW, "bfloat16"), "lw": sb(NW), "xd": sb(ND, "bfloat16"),
-    "gt": sb(ND, "bfloat16"), "gb": sb(ND, "bfloat16"), "gbm": sb(ND, "bfloat16"), "gb1": sb(ND, "bfloat16"),
-    "snd": sb(4 * ND, "bfloat16"), "rf": sb(4 * ND, "bfloat16"),
-    "NEW0": sb(108), "NEW1": sb(108), "U0": sb(108, "uint16"), "U1": sb(108, "uint16"),
-    "cu": sb(M, "uint16"), "lo0": sb(M, "uint16"), "lo1": sb(M, "uint16"), "lv": sb(M, "uint16"),
-    "AA0": sb(108), "AA1": sb(108), "DF": sb(108), "MM": sb(108),
-    "Z0": sb(8 * M, "int32"), "Z1": sb(8 * M, "int32"), "zm": sb(6 * M), "zb": sb(6 * M),
-    "bid0": sb(M, "int32"), "bid1": sb(M, "int32"), "dv0": sb(M), "dv1": sb(M),
-    "st0": sb(M, "bfloat16"), "st1": sb(M, "bfloat16"), "adv": sb(M, "bfloat16"),
-    "s0": sb(M), "s1": sb(M), "s2": sb(M), "s3": sb(M), "s5": sb(M), "s6": sb(M), "s7": sb(M), "s8": sb(M),
-    "s9": sb(M), "sa": sb(M), "om": sb(E, "bfloat16"), "oy": sb(E, "bfloat16"),
+    "W": bf(WEND), "QW": bf(QB + 20 * NW), "KT": bf(O + E), "L": sb(LW), "IOT": sb(O + E), "ST": bf(288),
+    "ID": bf(8 * 128), "BD": bf(256), "stf": sb(288), "idf": sb(128), "bdf": sb(128), "kr": i32(32), "kc": i32(384),
+    "kp": bf(768), "kf": sb(384), "kd": sb(ND), "cc": sb(384), "ci": i32(384), "pi": i32(8), "pf": sb(8),
+    "jraw": sb(M), "jj": sb(M), "wa": bf(M), "wb": bf(M), "wc": bf(9 * M), "c64": bf(M), "c85": bf(M), "cz": bf(ND),
+    "c128": bf(NW), "q2": bf(NW), "cmp": bf(NW), "G": bf(NW), "Ee": bf(NW), "Rv": bf(NW), "Xn": bf(NW), "Kg": bf(NW),
+    "cmpb": bf(NW), "lw": sb(2048), "lx": sb(2 * NW), "lv": sb(64), "lt": sb(128), "li": i32(M), "lu": u16(M),
+    "g0": bf(ND), "gt": bf(ND), "gb": bf(ND), "se": bf(ND), "u2": bf(4 * ND), "mk": bf(2 * ND), "t1": bf(ND), "rp": bf(ND),
+    "vd": bf(ND), "snd": bf(4 * ND), "rf": bf(4 * ND), "rb": bf(4 * ND),
+    "aa": sb(M), "mm": sb(M), "LP": i32(2 * M), "U": u16(2 * M), "cu": u16(M), "vu0": u16(M), "vu1": u16(M),
+    "eu": u16(M), "lo0": u16(M), "lo1": u16(M), "gu": u16(12), "vv0": i32(M), "vv1": i32(M), "vv2": i32(M),
+    "bb0": i32(M), "bb1": i32(M), "bb2": i32(M), "st0": bf(M), "st1": bf(M), "sg": bf(M),
+    "s0": sb(M), "s1": sb(M), "s2": sb(M), "s3": sb(M), "bp": sb(M),
+    "Z0": i32(8 * M), "Z1": i32(8 * M), "zm": sb(6 * M), "zb": sb(6 * M),
     "pcnt": ("psum", [128, 512], "float32"), "pk": ("psum", [128, 512], "float32"),
     "pe": ("psum", [128, 1024], "float32"), "pcb": ("psum", [128, 512], "float32"),
-    "pav": ("psum", [128, 512], "float32"), "pst": ("psum", [128, 512], "float32"),
-    "pv": ("psum", [128, 512], "float32"),
+    "pm": ("psum", [128, 1024], "float32"), "pq": ("psum", [128, 512], "float32"),
 }
-NDMA = 25
+NDMA = 30
 SEMAPHORES = (["cv", "cs", "cp", "cg"] + ["d%d" % i for i in range(NDMA)] + ["fa%d" % i for i in range(4)]
               + ["ba%d" % i for i in range(4)] + ["fl%d" % i for i in range(4)] + ["bl%d" % i for i in range(4)])
 XCH = 4
@@ -88,6 +99,7 @@ def rank_program(g, core, T, topo):
     log = {}
     total = {}
     nd = [0]
+    held = []
 
     def wait(q, sem, val):
         if waited[q].get(sem, 0) < val:
@@ -116,19 +128,44 @@ def rank_program(g, core, T, topo):
         for b, lo, hi in reads:
             log.setdefault(b, []).append([lo, hi, 0, sem, val])
 
+    def emit(call):
+        if held:
+            held[-1].append(call)
+        else:
+            call()
+
+    def weave(*chains):
+        runs = []
+        for chain in chains:
+            held.append([])
+            chain()
+            runs.append(held.pop())
+        for k in range(max(len(x) for x in runs)):
+            for x in runs:
+                if k < len(x):
+                    emit(x[k])
+
     def op(q, fn, reads, writes):
-        order(q, reads, writes)
-        ins = fn(Q[q])
-        count[q] += 1
-        ins.then_inc(T.sem[csem[q]], 1)
-        note(reads, writes, csem[q], count[q])
+        def call():
+            order(q, reads, writes)
+            ins = fn(Q[q])
+            count[q] += 1
+            ins.then_inc(T.sem[csem[q]], 1)
+            note(reads, writes, csem[q], count[q])
+        emit(call)
+
+    def dmas(q, pairs, reads, writes):
+        def call():
+            order(q, reads, writes)
+            sem = "d%d" % nd[0]
+            nd[0] += 1
+            for out, in_ in pairs:
+                Q[q].dma_start(out, in_).then_inc(T.sem[sem], 16)
+            note(reads, writes, sem, 16 * len(pairs))
+        emit(call)
 
     def dma(q, out, in_, reads, writes):
-        order(q, reads, writes)
-        sem = "d%d" % nd[0]
-        nd[0] += 1
-        Q[q].dma_start(out, in_).then_inc(T.sem[sem], 16)
-        note(reads, writes, sem, 16)
+        dmas(q, [(out, in_)], reads, writes)
 
     def r(b, lo=0, hi=M):
         return (b, lo, hi)
@@ -157,8 +194,8 @@ def rank_program(g, core, T, topo):
     def ttg(out, win, off, b, o):
         op("v", lambda e: e.tensor_tensor(ap(out), ind(win, off), ap(b), o), [win, off, b], [out])
 
-    def act(out, a, func, bias=0.0, scale=1.0, also=()):
-        op("s", lambda e: e.activation(ap(out), ap(a), func, bias=bias, scale=scale), [a], [out] + list(also))
+    def act(out, a, func, bias=0.0, scale=1.0):
+        op("s", lambda e: e.activation(ap(out), ap(a), func, bias=bias, scale=scale), [a], [out])
 
     def actg(out, win, off, bias=0.0):
         op("s", lambda e: e.activation(ap(out), ind(win, off), F.Identity, bias=bias), [win, off], [out])
@@ -177,331 +214,432 @@ def rank_program(g, core, T, topo):
             return ins
         op("p", fn, [x for out, terms in groups for ab in terms for x in ab], [out for out, terms in groups])
 
-    def wrap(ps, src, n):
+    def wrap(ps, src, n, first):
+        out = r(ps, 0, n // 16)
+
+        def head(e):
+            for k, (a, b) in enumerate(first):
+                ins = e.matmul(ap(out), ap(a), ap(b), k == 0, False)
+            return ins
+
         def fn(e):
             for i in range(16):
-                ins = e.matmul(T[ps][:, 0:n // 16], T.ST[:, 128 * i:128 * i + 128], T[src][:, i:n:16], i == 0, i == 15)
+                lo = 16 - i + 143 * (i & 1)
+                ins = e.matmul(ap(out), T.ST[:, lo:lo + 128], T[src][:, i:n:16], False, i == 15)
             return ins
-        op("p", fn, [r("ST", 0, 2048), r(src, 0, n)], [r(ps, 0, n // 16)])
+        op("p", head, [x for ab in first for x in ab], [out])
+        op("p", fn, [r("ST", 0, 288), r(src, 0, n)], [r(ps + "w", 0, 1)])
+        emit(lambda: note([], [out], "cp", count["p"]))
 
-    def exchange(sign, src_buf, src_lo, land, land_lo, asem, lsem):
-        dsts = [T.cores[(rank + sign * (1 + h)) % N] for h in range(3)]
-        masks = engine_plan(topo, core, dsts)
-        order("g", [r(src_buf, src_lo, src_lo + ND)], [])
-        trs = []
-        for h in range(3):
-            rid, pid = topo.addr(dsts[h], core)
-            trs.append(RemoteDMATransfer(dst_ids=[DstId(rid=rid, pnc=pid)], dma_engine_mask=masks[h], remote_sem=T.sem[asem],
-                                         src=T[src_buf][:, src_lo + 64 * h:src_lo + 64 * h + 64],
-                                         dst=T[land][:, land_lo + 64 * h:land_lo + 64 * h + 64]))
-        g.remote_dma_fused(trs, local_sem=T.sem[lsem])
-        note([r(src_buf, src_lo, src_lo + ND)], [], lsem, sum(bits(x) for x in masks))
-        arrive = 0
-        for h in range(3):
-            s = (rank - sign * (1 + h)) % N
-            sd = [T.cores[(s + sign * (1 + k)) % N] for k in range(3)]
-            arrive += bits(engine_plan(topo, T.cores[s], sd)[h])
-        note([], [r(land, land_lo, land_lo + ND)], asem, arrive)
+    def exchange(sign, srcs, land, land_lo, asem, lsem):
+        def call():
+            dsts = [T.cores[(rank + sign * (1 + h)) % N] for h in range(3)]
+            masks = engine_plan(topo, core, dsts)
+            order("g", srcs, [])
+            trs = []
+            for h in range(3):
+                rid, pid = topo.addr(dsts[h], core)
+                trs.append(RemoteDMATransfer(
+                    dst_ids=[DstId(rid=rid, pnc=pid)], dma_engine_mask=masks[h], remote_sem=T.sem[asem],
+                    srcs=[T[b][:, lo + 64 * h:lo + 64 * h + 64] for b, lo, hi in srcs],
+                    dsts=[T[land][:, land_lo + 64 * h:land_lo + 64 * h + 64]], alu_op=2 if len(srcs) > 1 else 0))
+            g.remote_dma_fused(trs, local_sem=T.sem[lsem])
+            note(srcs, [], lsem, sum(bits(x) for x in masks))
+            arrive = 0
+            for h in range(3):
+                s = (rank - sign * (1 + h)) % N
+                sd = [T.cores[(s + sign * (1 + k)) % N] for k in range(3)]
+                arrive += bits(engine_plan(topo, T.cores[s], sd)[h])
+            note([], [r(land, land_lo, land_lo + ND)], asem, arrive)
+        emit(call)
 
-    Tt = r("W", TB, TB + E)
-    doors = r("W", TB, TB + ND)
-    gate0 = r("W", XB + ND, XB + 2 * ND)
-    eye, neg = r("ID", 0, 128), r("ID", 128, 256)
-    fneg, tmpd = r("pv", 128, 320), r("pv", 320, 512)
+    both, marks, vals = r("W", 0, WEND), r("W", 0, O + E), r("W", GAP, WEND)
+    mdoor, vdoor = r("W", O, O + ND), r("W", TV, TV + ND)
+    eye, neg, eyeb, negb, neg2, eyeq, eyea, eyez = [r("ID", 128 * i, 128 * i + 128) for i in range(8)]
+    zg, zd = r("pq", 128, 128 + ND), r("pcb", 128, 128 + ND)
 
-    dma("y", T.kc[:, 0:192], T.k0[:], [], [r("kc", 0, 192)])
-    dma("s", T.W[:, QB:QB + NR], T.q[:], [], [r("W", QB, QB + NR)])
+    def nw(t):
+        return NR if t < 2 else NW
+
+    def thr(t, lo, hi):
+        return r("QW", QB + 2 * NW * t + lo, QB + 2 * NW * t + hi)
+
+    dmas("y", [(T.kr[:, 16 * h:16 * h + 16], T.k0[h:8:2, 2 * ND:2 * ND + 512]) for h in range(2)], [], [r("kr", 0, 32)])
+    dma("s", T.kc[:, 192:384], T.k1[:], [], [r("kc", 192, 384)])
+    dma("s", ap(thr(0, 0, NR)), T.q[:], [], [thr(0, 0, NR)])
     cw = E // XCH
     for c in range(XCH):
-        dma("y" if c % 2 == 0 else "s", T.W[:, TB + c * cw:TB + (c + 1) * cw], T.x[:, c * cw:(c + 1) * cw], [],
-            [r("W", TB + c * cw, TB + (c + 1) * cw)])
-    dma("y", T.kc[:, 192:384], T.k1[:], [], [r("kc", 192, 384)])
+        dma("y" if c % 2 == 0 else "s", T.W[:, TV + c * cw:TV + (c + 1) * cw], T.x[:, c * cw:(c + 1) * cw], [],
+            [r("W", TV + c * cw, TV + (c + 1) * cw)])
+    dma("y", T.kc[:, 0:192], T.k0[:], [], [r("kc", 0, 192)])
     op("g", lambda e: e.iota(T.pi[:, 0:1], [[1, 1]], 0, 1), [], [r("pi", 0, 1)])
-    iota(r("g8", 0, 8), [[16, 8]], 0, 0)
-    iota(r("jraw"), [[16, M]], 0, 1)
     iota(r("idf", 0, 128), [[1, 128]], 0, -1)
-    fill(r("W", XB, XB + ND), -230)
-    fill(r("WQ", TB, TB + ND), 2)
-    fill(r("WQ", LOWB + NR, TB), 1)
-    fill(r("WQ", 0, ND), 1)
-    fill(r("W", LOWB, TB), -240)
-    fill(r("W", QB + NR, WEND), -132)
-    iota(r("IOT", 0, E), [[1, E]], 64, 0)
+    iota(r("stf", 0, 288), [[1, 2], [1, 144]], -16, 0)
+    iota(r("jraw"), [[16, M]], 0, 1)
+    fill(r("c85"), int(8.5 * BIG))
+    fill(r("W", 0, O), 0)
+    iota(r("wa"), [[16, M]], 0, 0)
+    iota(r("wc", 0, 9 * M), [[2 * NW, 9], [0, M]], QB + NW, 0)
+    fill(r("QW", 0, O), 0)
+    fill(r("c64"), O)
+    fill(r("W", GAP, TV), 0)
+    for t, lo in ((0, 0), (0, NW), (1, 0), (1, NW), (2, 0)):
+        fill(thr(t, lo + NR, lo + NW), 100)
+    fill(r("c128", 0, NW), -128)
+    fill(r("lv", 0, 64), 0)
+    fill(r("lw", 0, NW), 0)
     iota(r("bdf", 0, 128), [[16, 8], [0, 16]], 0, 0)
-    fill(r("m1", 0, NW), -1)
 
-    ms(r("KT", 0, 1024), 0.0)
-    ms(r("ST", 0, 2048), 0.0)
-    act(r("KT", 1024, 2048), r("KT", 0, 1024), F.Copy)
-    act(r("KT", 2048, E), r("KT", 0, 1024), F.Copy)
-    for c in range(3):
-        act(r("WQ", TB + ND + 960 * c, TB + ND + 960 * c + 960), r("KT", 0, 960), F.Identity, bias=1.0,
-            also=[r("KTz", c, c + 1)])
+    ts(eye, r("idf", 0, 128), 0.0, None, A.is_equal)
+    ms(r("KT", 0, O + E), 0.0)
     ts(r("pi", 1, 2), r("pi", 0, 1), 112, None, A.bitwise_and)
     ts(r("pi", 2, 3), r("pi", 0, 1), 14, None, A.bitwise_and)
     ts(r("pi", 3, 4), r("pi", 0, 1), 15, None, A.bitwise_and)
+    ms(r("W", O + ND, O + 768), 0.0)
     cp(r("pf", 0, 3), r("pi", 1, 4))
-    ts(r("b8", 0, 8), r("g8", 0, 8), T.pf[:, 0:1], None, A.is_equal, extra=[r("pf", 0, 1)])
-    ts(r("pf", 6, 7), r("pf", 2, 3), 2.0, None, A.is_equal)
-    ts(r("pf", 7, 8), r("pf", 2, 3), 3.0, None, A.is_equal)
-    for i in range(16):
-        op("v", lambda e: e.tensor_copy(T.ST[:, 129 * i:128 * i + 128:16], T.b8[:, :]), [r("b8", 0, 8)],
-           [r("ST", 128 * i, 128 * i + 128)])
-    ts(r("klo", 0, 192), r("kc", 0, 192), 63, None, A.bitwise_and)
+    act(eyeb, eye, F.Silu, scale=B)
+    for m_, c in ((negb, -B), (neg, -1.0), (neg2, -2.0), (eyeq, -NW / B), (eyea, 16 * BIG), (eyez, 2176.0)):
+        act(m_, eye, F.Copy, scale=c)
+
+    def link_table(f):
+        lo = 192 * f
+        cp(r("kp", 384 + lo, 576 + lo), r("kc", lo, lo + 192))
+        tt(r("kp", lo, lo + 192), r("kc", lo, lo + 192), r("kp", 384 + lo, 576 + lo), A.subtract)
+        dmas("y", [(T.KT[2 * f + h:128:16, O:O + E], T.kp[:, 384 * h + lo:384 * h + lo + 192]) for h in range(2)],
+             [r("kp", lo, lo + 192), r("kp", 384 + lo, 576 + lo)], [r("KT", 0, O + E)])
+
+    def first_list():
+        ts(r("s3", 0, 32), r("kr", 0, 32), float(O), None, A.add)
+        op("v", lambda e: e.transpose(T.aa[:, 0:32], T.s3[:, 0:32]), [r("s3", 0, 32)], [r("aa", 0, 32)])
+        cp(r("cu", 0, 24), r("aa", 0, 24))
+
+    ts(r("ST", 0, 288), r("stf", 0, 288), T.pf[:, 0:1], -BIG, A.is_equal, A.mult, extra=[r("pf", 0, 1)])
     ts(r("jj"), r("jraw"), T.pf[:, 0:1], None, A.subtract, extra=[r("pf", 0, 1)])
-    cp(r("kp", 0, 192), r("klo", 0, 192))
-    tt(r("kp", 384, 576), r("kc", 0, 192), r("klo", 0, 192), A.subtract)
-    for n, (lo, col) in enumerate(((0, 6), (0, 7), (384, 6), (384, 7))):
-        ts(r("kz", 192 * n, 192 * n + 192), r("kp", lo, lo + 192), T.pf[:, col:col + 1], None, A.mult, extra=[r("pf", 6, 8)])
-    wrap("pk", "kz", 768)
-    ts(r("W", XB + ND, XB + 768), r("W", TB + ND, TB + 768), -128.0, None, A.add)
-    ts(r("klo", 192, 384), r("kc", 192, 384), 63, None, A.bitwise_and)
-    ts(r("W", QB, QB + NR), r("W", QB, QB + NR), -192.0, None, A.add)
-    cp(r("W", TB + ND, TB + 768), r("W", XB + ND, XB + 768))
-    cp(r("kp", 192, 384), r("klo", 192, 384))
-    cp(r("AA0", 0, 24), r("pk", 0, 24))
-    tt(r("kp", 576, 768), r("kc", 192, 384), r("klo", 192, 384), A.subtract)
-    tt(r("AA0", 0, 24), r("AA0", 0, 24), r("pk", 24, 48), A.add)
-    ts(r("NEW1", 0, 24), r("jj", 0, 24), 384.0, None, A.add)
-    cp(r("cu", 0, 24), r("AA0", 0, 24))
-    for row, lo in ((2, 192), (3, 576), (0, 0), (1, 384)):
-        dma("y", T.KT[row:128:16, :], T.kp[:, lo:lo + 192], [r("kp", lo, lo + 192), r("KT", 0, E), r("KTz", 0, 3)],
-            [r("KTr", row, row + 1)])
+    weave(lambda: link_table(1), first_list)
+    ts(thr(0, 0, NR), thr(0, 0, NR), 64.0, None, A.add)
+    ts(mdoor, vdoor, 64.0, None, A.add)
     for c in range(1, XCH):
-        act(r("W", XB + c * cw, XB + (c + 1) * cw), r("W", TB + c * cw, TB + (c + 1) * cw), F.Identity, bias=-128.0)
+        ts(r("W", O + c * cw, O + (c + 1) * cw), r("W", TV + c * cw, TV + (c + 1) * cw), 64.0, None, A.add)
+    for c in range(XCH):
+        act(r("QW", O + c * cw, O + (c + 1) * cw), r("W", TV + c * cw, TV + (c + 1) * cw), F.Identity, bias=62.0)
+        if c == 2:
+            act(r("Xn", 0, NR), r("W", TV + 2 * ND, TV + 2 * ND + NR), F.Copy)
 
     def setup_lists():
-        act(r("xd", 0, ND), doors, F.Identity, bias=-128.0)
-        ts(r("NEW1", 24, M), r("jj", 24, M), -192.0, None, A.add)
-        ts(eye, r("idf", 0, 128), 0.0, None, A.is_equal)
-        ms(r("AA0", 24, M), 0.0)
-        ms(r("adv"), 0.0)
-        ts(r("Z0", 2 * M, 3 * M), r("NEW1"), 8192.0, None, A.add)
-        ts(r("Z0", 3 * M, 4 * M), r("NEW1"), 8192.0, None, A.add)
-        cp(r("AA0", 72, 108), r("jj"))
-        ts(r("qsj"), r("jj"), float(QB - TB), None, A.add)
-        ts(neg, r("idf", 0, 128), 0.0, -1.0, A.is_equal, A.mult)
-        ts(r("pf", 4, 5), r("pf", 1, 2), 0.0, None, A.is_equal)
-        ts(r("pf", 5, 6), r("pf", 1, 2), 2.0, None, A.is_equal)
+        ts(r("vv0", 0, 24), r("jj", 0, 24), float(2 * ND + O), None, A.add)
+        ts(r("vv0", 24, M), r("jj", 24, M), float(O - ND), None, A.add)
+        ts(r("wb"), r("jraw"), 0.0, T.pf[:, 2:3], A.mult, A.add, extra=[r("pf", 2, 3)])
+        for b in (2, 3):
+            ts(r("Z0", b * M, b * M + M), r("vv0"), float(GAP + 2 * TURN), None, A.add)
+        ts(r("LP", 24, M), r("vv0", 24, M), float(GAP), None, A.add)
+        ms(r("LP", M + 24, 2 * M), 0)
+        ms(r("sg", 24, M), -1.0)
+        ts(r("pf", 4, 5), r("pf", 1, 2), 0.0, -1.0 / BIG, A.is_equal, A.mult)
+        ts(r("pf", 5, 6), r("pf", 1, 2), 2.0, -1.0 / BIG, A.is_equal, A.mult)
 
     def setup_links():
         mm([(r("pe", 0, 384), [(eye, r("kp", 0, 384)), (eye, r("kp", 384, 768))])])
-        act(r("kf", 0, 384), r("pe", 0, 384), F.Identity, bias=64.0)
-        dma("y", T.L[0:128:16, 0:E], T.kf[:, 0:192], [r("kf", 0, 192)], [r("L", 0, E)])
-        dma("y", T.L[0:128:16, 4096:4096 + E], T.kf[:, 192:384], [r("kf", 192, 384)], [r("L", 4096, 4096 + E)])
+        act(r("kf", 0, 384), r("pe", 0, 384), F.Identity, bias=float(O))
+        dmas("y", [(T.L[0:128:16, TV + TURN * f:TV + TURN * f + E], T.kf[:, 192 * f:192 * f + 192]) for f in range(2)],
+             [r("kf", 0, 384)], [r("L", 0, LW)])
 
-    def setup_guests():
-        actg(r("gt", 0, ND), r("W", XB, XB + E), r("cu", 24, M), bias=-1.0)
+    def setup_stack():
         for b in (3, 4, 5, 6):
             cp(r("Z1", b * M, b * M + M), r("Z0", 3 * M, 4 * M))
-        ts(r("AA1", 72, 108), r("jj"), float(LOWB), None, A.add)
         cp(r("Z0", 4 * M, 8 * M), r("Z1", 3 * M, 7 * M))
-        ts(r("BD", 0, 128), r("bdf", 0, 128), T.pf[:, 0:1], 300.0, A.is_equal, A.mult, extra=[r("pf", 0, 1)])
-        ts(r("BD", 128, 256), r("bdf", 0, 128), T.pf[:, 0:1], -150.0, A.is_equal, A.mult, extra=[r("pf", 0, 1)])
+
+    def setup_guests():
+        ts(r("s0", 0, 12), r("aa", 24, M), float(O + ND), None, A.is_ge)
+        ts(r("BD", 0, 128), r("bdf", 0, 128), T.pf[:, 0:1], 256.0, A.is_equal, A.mult, extra=[r("pf", 0, 1)])
+        tt(r("s1", 0, 12), r("s0", 0, 12), r("aa", 24, M), A.mult)
+        ts(r("BD", 128, 256), r("bdf", 0, 128), T.pf[:, 0:1], -256.0, A.is_equal, A.mult, extra=[r("pf", 0, 1)])
+        cp(r("gu", 0, 12), r("s1", 0, 12))
+        act(r("g0", 0, ND), r("QW", O + ND, O + 2 * ND), F.Identity, bias=-62.0)
+        actg(r("gt", 0, ND), r("QW", 0, O + E), r("gu", 0, 12), bias=-63.0)
         cp(r("kd", 0, ND), r("kc", 0, ND))
-        dma("y", T.yk0[:, 0:ND], T.kd[0:128:16, :], [r("kd", 0, ND)], [])
-        dma("y", T.yk1[:, 0:ND], T.kd[0:128:16, :], [r("kd", 0, ND)], [])
-        tt(r("gb", 0, ND), r("gt", 0, ND), gate0, A.max)
-        ts(r("gbm", 0, ND), r("gb", 0, ND), -150.0, None, A.add)
+        dmas("y", [(T.yk0[:, 0:ND], T.kd[0:128:16, :]), (T.yk1[:, 0:ND], T.kd[0:128:16, :])], [r("kd", 0, ND)], [])
 
-    def kgather(t, ub):
+    def named(t):
+        cp(r("cu", 0, nw(t) // 16), r("pk", 0, nw(t) // 16))
+        act(r("aa", 0, nw(t) // 16), r("pk", 0, nw(t) // 16), F.Copy)
+
+    def compare(t, lo, hi):
+        ttg(r("cmp", lo, hi), marks, r("cu", lo // 16, hi // 16), thr(t, lo, hi), A.is_ge)
+
+    def countw(t):
+        m = nw(t) // 16
+        wrap("pcnt", "cmp", nw(t), [(eye, r("c85", 0, m))])
+
+    def before(t):
         f = t & 1
-        op("s", lambda e: e.activation(T.Kg[:, :], ind(r("KT", 0, E), r(ub)), F.Copy, scale=T.pf[:, 4 + f:5 + f]),
-           [r("KT", 0, E), r(ub), r("pf", 4, 6), r("KTr", 0, 4)], [r("Kg", 0, NW)])
-        wrap("pk", "Kg", NW)
-
-    def links(t):
-        bid, dv = "bid%d" % (t & 1), "dv%d" % (t & 1)
-        n = NR if t < 2 else NW
-        m = n // 16
-        if t == 0:
-            cp(r("lv"), r(bid))
-        else:
-            ts(r("s6", 0, m), r("pcb", 0, m), 9.0 if t == 9 else 1.0, None, A.is_ge)
-            tt(r("s7", 0, m), r("s6", 0, m), r(dv, 0, m), A.mult)
-            tt(r("s8", 0, m), r("s7", 0, m), r(bid, 0, m), A.add)
-            cp(r("lv", 0, m), r("s8", 0, m))
-        actg(r("lw", 0, n), r("IOT", 0, E), r("lv", 0, m))
-        lo = r("lo%d" % (t & 1), 0, m)
-        op("s", lambda e: e.activation(ind(r("L", 0, LW), lo), T.lw[:, 0:n], F.Silu), [lo, r("lw", 0, n)], [r("L", 0, LW)])
+        v, b, st = r("vv%d" % (t % 3)), r("bb%d" % (t % 3)), r("st%d" % f)
+        if t > 0:
+            if f == 0 or t == 1:
+                ts(st, v, float(O + ND), B, A.is_lt, A.mult)
+            else:
+                ts(r("s0"), v, float(O + ND), B, A.is_lt, A.mult)
+        ts(b, r("Z%d" % f, 2 * M, 3 * M), TURN - 1, None, A.bitwise_and)
+        if f == 1 and t > 1:
+            tt(st, r("s0"), r("st0"), A.subtract)
+        ts(r("Z%d" % f), v, float(GAP + TURN * f), None, A.add)
+        if f == 1:
+            ts(r("eu"), b, float(-GAP), None, A.add)
+        if t > 0:
+            tt(r("s1"), b, st, A.subtract)
+        ts(r("Z%d" % f, M, 2 * M), v, float(GAP + TURN * f), None, A.add)
+        if t > 0:
+            tt(r("bp"), r("s1"), v, A.max)
+        if t > 0 and f == 0:
+            cp(r("eu"), r("bp"))
+        if t < 9:
+            mm([(r("pq"), [(eye, r("wa")), (eye, r("wb")), (eye, r("wc", M * t, M * t + M))]
+                 + ([(eyeq, st)] if t > 0 else []))])
 
     def depth(t):
         return min(t + 1, 9 - t) + 1
 
+    def decide(t):
+        m, f = nw(t) // 16, t & 1
+        st, k = r("st%d" % f), depth(t)
+        tt(r("mm", 0, m), r("aa", 0, m), r("pcnt", 0, m), A.max)
+        act(r("sg", 0, m), r("pcnt", 0, m), F.Sign, scale=-1.0)
+        tt(r("LP", 0, m), r("mm", 0, m), r("bp" if t else "bb0", 0, m), A.min)
+        if t < 9:
+            tt(r("LP", M, M + m), r("mm", 0, m), r("pq", 0, m), A.min)
+            ts(r("vv%d" % ((t + 1) % 3)), r("LP"), GAP - 1, None, A.bitwise_and)
+            cp(r("U", 0, 2 * M), r("LP", 0, 2 * M))
+            cp(r("vu%d" % (1 - f)), r("vv%d" % ((t + 1) % 3)))
+        else:
+            cp(r("U"), r("LP"))
+        mm([(r("pm", M * j, M * j + M), [(eyeb, r("sg"))]) for j in range(k)]
+           + [(r("pm", 256 + M * j, 256 + M * j + M), [(eye, st)]) for j in range(k) if t > 0]
+           + [(r("pm", 512 + M * j, 512 + M * j + M), [(negb, r("sg"))] + ([(neg2, st)] if t > 0 else [])) for j in range(k)])
+
+    def thresholds(t):
+        n = nw(t)
+        ttg(thr(t + 1, 0, n), r("QW", 0, QB + 2 * NW * (t + 1)), r("U", M, M + n // 16), r("q2", 0, n), A.max)
+
+    def lowered(t):
+        n = nw(t)
+        act(r("q2", 0, n), thr(t, 0, n), F.Identity, bias=-2.0)
+        act(thr(t, NW, NW + n), thr(t, 0, n), F.Identity, bias=-1.0)
+
+    def kgather(t):
+        f, n = t & 1, nw(t)
+        vu = r("vu%d" % f, 0, n // 16)
+        op("s", lambda e: e.activation(T.Kg[:, 0:n], ind(r("KT", 0, O + E), vu), F.Copy, scale=T.pf[:, 4 + f:5 + f]),
+           [r("KT", 0, O + E), vu, r("pf", 4, 6)], [r("Kg", 0, n)])
+        wrap("pk", "Kg", n, [(eye, r("c64", 0, n // 16))])
+
+    def scatter(t, a, b=None):
+        u = r("U", 0, nw(t) // 16)
+        if b is None:
+            op("v", lambda e: e.tensor_copy(ind(both, u), ap(a)), [u, a], [both])
+        else:
+            op("v", lambda e: e.tensor_tensor(ind(both, u), ap(a), ap(b), A.add), [u, a, b], [both])
+
+    def here(t):
+        actg(r("G", 0, nw(t)), vals, r("vu%d" % (t & 1), 0, nw(t) // 16), bias=-1.0)
+
+    def differ(n, a, b):
+        mm([(r("pe", lo, hi), [(eye, r(a, lo, hi)), (neg, r(b, lo, hi))]) for lo, hi in ((0, min(n, 512)), (512, n)) if hi > lo])
+
+    def countb(t):
+        m = nw(t) // 16
+        wrap("pcb", "cmpb", nw(t), [(eye, r("c85", 0, m)), (eye, r("c85", 0, m)), (eyea, r("sg", 0, m))])
+
     def stack(t):
         f = t & 1
-        zo, zn, zw, v = "Z%d" % f, "Z%d" % (1 - f), M * depth(t), r("NEW%d" % (1 - f))
-        ts(r(zo), v, float(4096 * f), None, A.add)
-        ts(r(zo, M, 2 * M), v, float(4096 * f), None, A.add)
-        tt(r("zm", 0, zw), r(zo, 2 * M, 2 * M + zw), r("pav", 256, 256 + zw), A.mult)
-        tt(r("pav", 0, zw), r(zo, 0, zw), r("pav", 0, zw), A.mult)
+        zo, zn, zw = "Z%d" % f, "Z%d" % (1 - f), M * depth(t)
+        tt(r("zm", 0, zw), r(zo, 2 * M, 2 * M + zw), r("pm", 512, 512 + zw), A.min)
+        tt(r("pm", 0, zw), r(zo, 0, zw), r("pm", 0, zw), A.min)
         if t > 0:
-            tt(r("zb", 0, zw), r(zo, M, M + zw), r("pst", 0, zw), A.mult)
-            tt(r("pav", 0, zw), r("zm", 0, zw), r("pav", 0, zw), A.add)
-            tt(r(zn, M, M + zw), r("zb", 0, zw), r("pav", 0, zw), A.add)
+            tt(r("zb", 0, zw), r(zo, M, M + zw), r("pm", 256, 256 + zw), A.min)
+            tt(r("pm", 0, zw), r("zm", 0, zw), r("pm", 0, zw), A.max)
+            tt(r(zn, M, M + zw), r("zb", 0, zw), r("pm", 0, zw), A.max)
         else:
-            tt(r(zn, M, M + zw), r("zm", 0, zw), r("pav", 0, zw), A.add)
+            tt(r(zn, M, M + zw), r("zm", 0, zw), r("pm", 0, zw), A.max)
         cp(r("lo%d" % f), r(zn, M, 2 * M))
 
-    for t in range(10):
-        f, ph = t & 1, t // 2
-        n = NR if t < 2 else NW
-        m = n // 16
-        thr = float(192 - 2 * t)
-        back = f == 1 and t >= 3
-        start = f == 0 and t >= 2
-        dq = f == 1 and t < 9
-        old, new, un = "NEW%d" % (1 - f), "NEW%d" % f, "U%d" % f
-        bid, dv, st = "bid%d" % f, "dv%d" % f, "st%d" % f
-        AA = "AA1" if back else "AA0"
-        v = r(old)
-        k = depth(t)
+    def link_values(t):
+        f, m = t & 1, nw(t) // 16
+        if t == 0:
+            cp(r("lv", 0, m), r("bb0", 0, m))
+        else:
+            tt(r("s2", 0, m), r("vv%d" % (t % 3), 0, m), r("pcb", 0, m), A.max)
+            tt(r("lv", 0, m), r("s2", 0, m), r("bb%d" % (t % 3), 0, m), A.min)
+        nb = (m + 31) // 32
+        lt = r("lt", 64 * f, 64 * f + 32 * nb)
+        op("v", lambda e: e.transpose(ap(lt), T.lv[:, 0:32 * nb]), [r("lv", 0, 64)], [lt])
+        dmas("y", [(T.lw[16 * h:128:32, 1024 * f + 512 * b:1024 * f + 512 * b + 512],
+                    T.lt[:, 64 * f + 32 * b + 16 * h:64 * f + 32 * b + 16 * h + 16]) for b in range(nb) for h in range(2)],
+             [lt], [r("lw", 1024 * f, 1024 * f + 1024)])
 
-        if t > 0:
-            cp(r("cu"), r("pk"))
-        if start:
-            ttg(r("D", 0, NR), Tt, r("cu", 0, 24), r("W", QB, QB + NR), A.subtract)
-            ts(fneg, doors, -140.0, -300.0, A.is_ge, A.mult)
-            if t == 2:
-                setup_guests()
-            if t == 8:
-                cp(r("W", XB, XB + ND), r("xd", 0, ND))
+    def link_write(t):
+        f, n = t & 1, nw(t)
+        lo, lw = r("lo%d" % f, 0, n // 16), r("lw", 1024 * f, 1024 * f + n)
+        op("s", lambda e: e.activation(ind(r("L", 0, LW), lo), ap(lw), F.Silu), [lo, lw], [r("L", 0, LW)])
+
+    def exact_write(t):
+        tt(r("s2"), r("vv%d" % (t % 3)), r("pcb"), A.max)
+        tt(r("li"), r("s2"), r("bb%d" % (t % 3)), A.min)
+        ts(r("li"), r("li"), GAP - 1, None, A.bitwise_and)
+        cp(r("lu"), r("li"))
+        actg(r("lx", NW * (t & 1), NW * (t & 1) + NW), r("IOT", 0, O + E), r("lu"))
+
+    def exact_scatter(t):
+        lo, lx = r("lo%d" % (t & 1)), r("lx", NW * (t & 1), NW * (t & 1) + NW)
+        op("v", lambda e: e.tensor_copy(ind(r("L", 0, LW), lo), ap(lx)), [lo, lx], [r("L", 0, LW)])
+
+    def link_rows(f):
+        return T.L[0:128:16, TV + TURN * f + ND:TV + TURN * f + E]
+
+    def guests_retreat():
+        mm([(zg, [(eyez, r("se", 0, ND)), (r("BD", 128, 256), r("cmp", NR, NW))])])
+
+    def guests_back(ph):
+        u2, snd = r("u2", ND * (ph - 1), ND * ph), r("snd", ND * (ph - 1), ND * ph)
+        tt(u2, r("gb", 0, ND), zg, A.min)
+        if not FOLD:
+            tt(snd, u2, r("g0", 0, ND), A.max)
+        exchange(-1, [u2, r("g0", 0, ND)] if FOLD else [snd], "rb", ND * (ph - 1), "ba%d" % (ph - 1), "bl%d" % (ph - 1))
+
+    def waiting(ph):
+        return r("mk", ND * (ph & 1), ND * (ph & 1) + ND)
+
+    def doors_take(ph):
+        tt(r("t1", 0, ND), r("rb", ND * (ph - 1), ND * ph), waiting(ph - 1), A.min)
+        tt(vdoor, r("vd", 0, ND), r("t1", 0, ND), A.max)
+
+    def doors_clear(ph):
+        mm([(zd, [(eye, vdoor), (neg, waiting(ph))])])
+        act(r("vd", 0, ND), zd, F.Relu)
+
+    compare(0, 0, NR)
+    countw(0)
+    setup_lists()
+    before(0)
+    lowered(0)
+    for ph in range(5):
+        t = 2 * ph
+        n = nw(t)
+        wide = [r(b, 0, n) for b in ("Xn", "Ee", "Rv", "cmpb", "pe")]
+        if ph > 0:
+            here(t)
+            if EVEN_ON_SCALAR:
+                actg(wide[1], both, r("eu"))
+                differ(n, "G", "Ee")
+            tt(thr(t, NR, NW), thr(t, NR, NW), r("rp", 0, ND), A.min)
+            compare(t, NR, NW)
+            countw(t)
+            mm([(zg, [(neg, r("cz", 0, ND)), (r("BD", 0, 128), r("cmp", NR, NW))])])
+            if EVEN_ON_SCALAR:
+                act(wide[2], wide[4], F.Relu)
+            lowered(t)
+            link_values(t - 1)
+            if not EVEN_ON_SCALAR:
+                ttg(wide[0], both, r("eu"), r("G", 0, n), A.max)
+                differ(n, "Xn", "G")
+        decide(t)
+        kgather(t + 1)
+        if ph > 0 and EVEN_ON_SCALAR:
+            scatter(t, wide[1], wide[2])
+        else:
+            scatter(t, wide[0])
+        thresholds(t)
+        if ph == 0:
+            link_table(0)
+            setup_stack()
+        else:
+            act(r("se", 0, ND), zg, F.Sign)
+            act(wide[3], wide[4], F.Sign, bias=1.5, scale=1.0 if EVEN_ON_SCALAR else -1.0)
+            if ph == 1:
+                tt(r("gb", 0, ND), r("gt", 0, ND), r("g0", 0, ND), A.max)
+            doors_clear(ph - 1)
+        t += 1
+        if ph == 4:
+            break
+        named(t)
+        compare(t, 0, n)
+        if ph > 0:
+            guests_retreat()
+        countw(t)
+        lowered(t)
+        if ph > 0:
+            link_write(t - 2)
+            countb(t - 1)
+            weave(lambda: stack(t - 1), lambda: guests_back(ph))
+        else:
             stack(t - 1)
-            act(r("cmp", 0, NR), r("D", 0, NR), F.Sign, bias=0.5 - thr)
-            tt(r("W", QB + NR, WEND), r("W", QB + NR, WEND), r("rf", ND * (ph - 1), ND * ph), A.min)
-            ttg(r("D", NR, NW), Tt, r("cu", 24, M), r("W", QB + NR, WEND), A.subtract)
-            ts(r("cmp", NR, n), r("D", NR, n), thr, 0.5, A.is_ge, A.subtract)
-        else:
-            ttg(r("D", 0, n), Tt, r("cu", 0, m), r("W", QB, QB + n), A.subtract)
-            if t == 0:
-                ts(r("cmp", 0, n), r("D", 0, n), thr, 0.5, A.is_ge, A.subtract)
-            else:
-                act(r("cmp", 0, n), r("D", 0, n), F.Sign, bias=0.5 - thr)
-        if back:
-            mm([(r("pe", 0, ND), [(eye, r("gb1", 0, ND)), (r("BD", 128, 256), r("cmp", NR, NW))])])
-        wrap("pcnt", "cmp", n)
-        if t < 9:
-            act(r("WQ", LOWB, LOWB + n), r("D", 0, n), F.Relu, bias=-thr)
-        if t >= 2:
-            wrap("pcb", "cmpb", NR if t - 1 < 2 else NW)
-        if t == 0:
-            setup_lists()
-        elif not start:
-            stack(t - 1)
-        if back:
-            tt(r("pe", 0, ND), r("gb1", 0, ND), r("pe", 0, ND), A.min)
-            tt(r("snd", ND * (ph - 1), ND * ph), gate0, r("pe", 0, ND), A.max)
-            exchange(-1, "snd", ND * (ph - 1), "W", 0, "ba%d" % (ph - 1), "bl%d" % (ph - 1))
-        if t > 0:
-            cp(r(AA), r("pk"))
-        ts(r(bid), r("Z%d" % f, 2 * M, 3 * M), 4095, None, A.bitwise_and)
-        if f == 0:
-            ts(r(st), v, 192.0, None, A.is_lt)
-        else:
-            ts(r("s0"), v, 192.0, None, A.is_lt)
-        if dq:
-            ts(r("s2"), r(AA), 192.0, None, A.is_lt)
-        if f == 1:
-            tt(r(st), r("s0"), r("st0"), A.subtract)
-        tt(r(dv), v, r(bid), A.subtract)
-        if back:
-            ts(r("s9"), r("st0"), -float(TB), float(TB), A.mult, A.add)
-        else:
-            ts(r("pv", 72, 108), v, float(OB), None, A.add)
-        if dq:
-            ts(r("s3"), r(AA), float(E), None, A.add)
-            tt(r("sa"), r("s2"), r("qsj"), A.mult)
-            tt(r("s5"), r(st), r("qsj"), A.mult)
-        else:
-            ts(r(AA, M, 72), r(AA), float(E), None, A.add)
-        tt(r("s1"), r(st), r(dv), A.mult)
-        if back:
-            tt(r("pv", 72, 108), r("s9"), v, A.add)
-        if dq:
-            tt(r(AA, M, 72), r("sa"), r("s3"), A.max)
-            tt(r("pv", M, 72), r("s5"), r(bid), A.max)
-        else:
-            tt(r("pv", M, 72), r("s1"), r(bid), A.add)
-        tt(r("pv"), r("s1"), r(bid), A.add)
-        tt(r("DF", 0, 108), r(AA, 0, 108), r("pv", 0, 108), A.subtract)
-        ts(r("adv", 0, m), r("pcnt", 0, m), 0.75, None, A.is_ge)
-        for j in range(3):
-            tt(r("MM", M * j, M * j + M), r("DF", M * j, M * j + M), r("adv"), A.mult)
-        tt(r(new, 0, 108), r("MM", 0, 108), r("pv", 0, 108), A.add)
-        cp(r(un, 0, 108), r(new, 0, 108))
-        if start:
-            mm([(r("pcnt", 0, ND), [(eye, r("gbm", 0, ND)), (r("BD", 0, 128), r("cmp", NR, NW))])])
-        mm([(r("pav", M * j, M * j + M), [(eye, r("adv"))]) for j in range(k)]
-           + [(r("pav", 256 + M * j, 256 + M * j + M), [(eye, r("WQ")), (neg, r("adv")), (neg, r(st))]) for j in range(k)])
-        if t > 0:
-            mm([(r("pst", M * j, M * j + M), [(eye, r(st))]) for j in range(k)])
-        vl, off1, o_list = r(un, 0, m), r(un, M, M + m), r(un, 72, 72 + m)
-        w0 = 0 if back else LOWB
-        wold = r("W", w0, TB + E)
-        wnew = r("W", TB, WEND if dq else QB)
-        if back:
-            if t < 9:
-                kgather(t + 1, un)
-        elif t > 0:
-            actg(r("G", 0, n), wold, o_list, bias=-1.0)
-        if t < 9:
-            ttg(r("W", QB, QB + n), r("WQ", w0, TB + E), o_list, r("W", QB, QB + n), A.add)
-        if back:
-            if t == 9:
-                actg(r("Y0", 0, n), wnew, off1)
-            actg(r("Y", 0, n), wnew, off1, bias=1.0)
-            if t < 9:
-                actg(r("G", 0, n), wold, o_list, bias=-1.0)
-        else:
-            kgather(t + 1, un)
-        if t >= 1:
-            links(t - 1)
-        if start:
-            tt(r("gb1", 0, ND), r("gb", 0, ND), r("pcnt", 0, ND), A.min)
-        if back:
-            if t == 9:
-                stack(9)
-            tt(tmpd, r("W", 0, ND), fneg, A.add)
-            if t == 9:
-                ttg(r("cmpb", 0, n), wold, o_list, r("Y0", 0, n), A.is_ge)
-                wrap("pcb", "cmpb", NW)
-            ttg(r("Xn", 0, n), wold, o_list, r("Y", 0, n), A.max)
-            tt(doors, doors, tmpd, A.max)
-            if t == 9:
-                links(9)
-            op("v", lambda e: e.tensor_tensor(ind(Tt, vl), T.Xn[:, 0:n], T.m1[:, 0:n], A.add),
-               [vl, r("Xn", 0, n), r("m1", 0, n)], [Tt])
-        else:
-            if t == 0:
-                op("v", lambda e: e.tensor_copy(T.Xn[:, 0:n], ind(wnew, off1)), [wnew, off1], [r("Xn", 0, n)])
-            else:
-                ttg(r("Xn", 0, n), wnew, off1, r("G", 0, n), A.max)
-            op("v", lambda e: e.tensor_copy(ind(Tt, vl), T.Xn[:, 0:n]), [vl, r("Xn", 0, n)], [Tt])
-        if dq:
-            exchange(1, "W", TB, "rf", ND * ph, "fa%d" % ph, "fl%d" % ph)
-        if 1 <= t < 9:
-            mm([(r("pe", lo, hi), [(eye, r("Xn", lo, hi)), (neg, r("G", lo, hi))])
-                for lo, hi in ((0, min(n, 512)), (512, n)) if hi > lo])
-            act(r("cmpb", 0, n), r("pe", 0, n), F.Sign, bias=2.5 if back else 1.5, scale=-1.0)
-        if t == 0:
+        before(t)
+        actg(wide[1], vals, r("eu", 0, n // 16))
+        if ph == 0:
+            here(t)
+        decide(t)
+        thresholds(t)
+        kgather(t + 1)
+        scatter(t, thr(t + 1, 0, n), r("c128", 0, n))
+        exchange(1, [mdoor], "rf", ND * ph, "fa%d" % ph, "fl%d" % ph)
+        if ph == 0:
+            fill(r("cz", 0, ND), 2176)
+            fill(r("W", O + E, GAP), 0)
+            fill(r("lw", 1024, 1024 + NW), 0)
             setup_links()
-
-    dma("s", T.cc[:, 0:CW], T.L[0:128:16, ND:E], [r("L", 0, E)], [r("cc", 0, CW)])
-    dma("s", T.cc[:, CW:2 * CW], T.L[0:128:16, 4096 + ND:4096 + E], [r("L", 4096, 4096 + E)], [r("cc", CW, 2 * CW)])
-    banks = [("pcnt", 0), ("pe", 0), ("pk", 0), ("pe", 512), ("pav", 0), ("pst", 0)]
-    for c, (ps, p0) in enumerate(banks):
-        lo, hi = 512 * c, 512 * c + 512
-        src, bank = r("W", TB + lo, TB + hi), r(ps, p0, p0 + 512)
-        if c % 2 == 0:
-            mm([(bank, [(eye, src)])])
-            ts(r("om", lo, hi + 512), r("W", TB + lo, TB + hi + 512), 0.0, 128.0, A.is_lt, A.mult)
-            tt(r("oy", lo, hi), r("om", lo, hi), bank, A.add)
+        elif ph < 3:
+            lo = (O + E) // 2 * (ph - 1)
+            iota(r("IOT", lo, lo + (O + E) // 2), [[1, (O + E) // 2]], lo - O, 0)
         else:
-            mm([(bank, [(eye, src), (eye, r("om", lo, hi))])])
-            act(r("oy", lo, hi), bank, F.Copy)
-        dma("y" if c % 2 == 0 else "s", T.yx[:, lo:hi], T.oy[:, lo:hi], [r("oy", lo, hi)], [])
-    ts(r("kf", 0, 2 * CW), r("cc", 0, 2 * CW), MAGIC, MAGIC + 64.0, A.add, A.subtract)
-    dma("y", T.yk0[:, ND:E], T.kf[:, 0:CW], [r("kf", 0, CW)], [])
-    dma("s", T.yk1[:, ND:E], T.kf[:, CW:2 * CW], [r("kf", CW, 2 * CW)], [])
+            fill(r("c128", 0, NW), -1)
+        if ph > 0:
+            weave(lambda: doors_take(ph), lambda: link_values(t - 1))
+            here(t)
+        else:
+            link_values(t - 1)
+        differ(n, "G", "Ee")
+        act(waiting(ph), mdoor, F.Relu, bias=-20.0, scale=-1.0)
+        act(wide[2], wide[4], F.Relu)
+        act(wide[3], wide[4], F.Sign, bias=1.5)
+        countb(t)
+        stack(t)
+        named(t + 1)
+        compare(t + 1, 0, NR)
+        if ph == 0:
+            setup_guests()
+        before(t + 1)
+        scatter(t, wide[1], wide[2])
+        act(r("rp", 0, ND), r("rf", ND * ph, ND * ph + ND), F.Identity, bias=128.0)
+        link_write(t - 1)
+
+    link_write(7)
+    dmas("y", [(T.cc[:, CW * f:CW * f + CW], link_rows(f)) for f in range(2)], [r("L", 0, LW)], [r("cc", 0, 2 * CW)])
+    named(9)
+    compare(9, NR, NW)
+    guests_retreat()
+    compare(9, 0, NR)
+    countw(9)
+    countb(8)
+    weave(lambda: guests_back(4), lambda: stack(8))
+    before(9)
+    actg(r("Ee", 0, NW), vals, r("eu"), bias=1.0)
+    decide(9)
+    weave(lambda: exact_write(8), lambda: stack(9))
+    cp(r("ci", 0, 2 * CW), r("cc", 0, 2 * CW))
+    ts(r("ci", 0, 2 * CW), r("ci", 0, 2 * CW), GAP - 1, None, A.bitwise_and)
+    ts(r("cc", 0, 2 * CW), r("ci", 0, 2 * CW), float(-O), None, A.add)
+    dmas("y", [(link_rows(f), T.cc[:, CW * f:CW * f + CW]) for f in range(2)], [r("cc", 0, 2 * CW)], [r("L", 0, LW)])
+    doors_take(4)
+    here(9)
+    ttg(r("Xn", 0, NW), vals, r("vu1"), r("Ee", 0, NW), A.max)
+    differ(NW, "G", "Ee")
+    act(r("cmpb", 0, NW), r("pe", 0, NW), F.Sign, bias=2.5)
+    countb(9)
+    scatter(9, r("Xn", 0, NW), r("c128", 0, NW))
+    for c in range(2):
+        dma("y" if c else "s", T.yx[:, 1536 * c:1536 * c + 1536], T.W[:, TV + 1536 * c:TV + 1536 * c + 1536], [vals], [])
+    exact_write(9)
+    exact_scatter(8)
+    exact_scatter(9)
+    dma("y", T.yk0[:, ND:E], link_rows(0), [r("L", 0, LW)], [])
+    dma("s", T.yk1[:, ND:E], link_rows(1), [r("L", 0, LW)], [])
     for sem in total:
         wait("y", sem, total[sem])

@@ -6,12 +6,16 @@ O = 64
 GAP = 4096
 TV, WEND = GAP + O, GAP + O + E
 TURN = 8192
-LW = 2 * TURN + GAP + O + 2 * ND + NR
+LW = 2 * TURN + O + 2 * ND + NR
 QB = O + E
 BIG, B = 65536.0, 32768.0
 CW = (E - ND) // 16
-FOLD = False
-EVEN_ON_SCALAR = False
+MAGIC = 12582912.0
+CYCLE, PE, GATHER, WAKE = 0.00095, 0.72, 1.5, 0.08
+SCATTER = 3.0
+REMOTE = 2.4
+LOCAL = 1.8
+PASSES = 2
 
 
 def sb(n, dtype="float32"):
@@ -32,25 +36,26 @@ def u16(n):
 
 SCRATCH = {
     "W": bf(WEND), "QW": bf(QB + 20 * NW), "KT": bf(O + E), "L": sb(LW), "IOT": sb(O + E), "ST": bf(288),
-    "ID": bf(8 * 128), "BD": bf(256), "stf": sb(288), "idf": sb(128), "bdf": sb(128), "kr": i32(32), "kc": i32(384),
-    "kp": bf(768), "kf": sb(384), "kd": sb(ND), "cc": sb(384), "ci": i32(384), "pi": i32(8), "pf": sb(8),
+    "ID": bf(9 * 128), "BD": bf(256), "stf": sb(288), "idf": sb(128), "bdf": sb(128), "kr": i32(32), "kc": i32(384),
+    "kp": bf(768), "kf": sb(384), "kd": sb(ND), "cc": sb(384), "cs": bf(384), "pi": i32(8), "pf": sb(8),
     "jraw": sb(M), "jj": sb(M), "wa": bf(M), "wb": bf(M), "wc": bf(9 * M), "c64": bf(M), "c85": bf(M), "cz": bf(ND),
-    "c128": bf(NW), "q2": bf(NW), "cmp": bf(NW), "G": bf(NW), "Ee": bf(NW), "Rv": bf(NW), "Xn": bf(NW), "Kg": bf(NW),
+    "c128": bf(NW), "m1": bf(NW),
+    "q2": bf(NW), "cmp": bf(NW), "G": bf(NW), "Ee": bf(NW), "Rv": bf(NW), "Xn": bf(NW), "Kg": bf(NW),
     "cmpb": bf(NW), "lw": sb(2048), "lx": sb(2 * NW), "lv": sb(64), "lt": sb(128), "li": i32(M), "lu": u16(M),
-    "g0": bf(ND), "gt": bf(ND), "gb": bf(ND), "se": bf(ND), "u2": bf(4 * ND), "mk": bf(2 * ND), "t1": bf(ND), "rp": bf(ND),
-    "vd": bf(ND), "snd": bf(4 * ND), "rf": bf(4 * ND), "rb": bf(4 * ND),
-    "aa": sb(M), "mm": sb(M), "LP": i32(2 * M), "U": u16(2 * M), "cu": u16(M), "vu0": u16(M), "vu1": u16(M),
-    "eu": u16(M), "lo0": u16(M), "lo1": u16(M), "gu": u16(12), "vv0": i32(M), "vv1": i32(M), "vv2": i32(M),
-    "bb0": i32(M), "bb1": i32(M), "bb2": i32(M), "st0": bf(M), "st1": bf(M), "sg": bf(M),
+    "g0": bf(ND), "gt": bf(ND), "gb": bf(ND), "se": bf(ND), "u2": bf(ND), "mk": bf(2 * ND), "t1": bf(ND),
+    "rp": bf(4 * ND), "vd": bf(ND), "snd": bf(4 * ND), "rf": bf(4 * ND), "rb": bf(4 * ND),
+    "aa": sb(M), "mm": sb(M), "P0": i32(3 * M), "P1": i32(3 * M), "P2": i32(3 * M), "U0": u16(3 * M), "U1": u16(3 * M),
+    "cu": u16(M), "EL0": u16(3 * M), "EL1": u16(3 * M), "gu": u16(12), "st0": bf(M), "st1": bf(M), "sg": bf(M),
     "s0": sb(M), "s1": sb(M), "s2": sb(M), "s3": sb(M), "bp": sb(M),
-    "Z0": i32(8 * M), "Z1": i32(8 * M), "zm": sb(6 * M), "zb": sb(6 * M),
+    "Z0": i32(9 * M), "Z1": i32(9 * M), "zm": sb(6 * M), "zb": sb(6 * M),
     "pcnt": ("psum", [128, 512], "float32"), "pk": ("psum", [128, 512], "float32"),
     "pe": ("psum", [128, 1024], "float32"), "pcb": ("psum", [128, 512], "float32"),
     "pm": ("psum", [128, 1024], "float32"), "pq": ("psum", [128, 512], "float32"),
 }
-NDMA = 30
+NDMA = 32
 SEMAPHORES = (["cv", "cs", "cp", "cg"] + ["d%d" % i for i in range(NDMA)] + ["fa%d" % i for i in range(4)]
               + ["ba%d" % i for i in range(4)] + ["fl%d" % i for i in range(4)] + ["bl%d" % i for i in range(4)])
+TURNS = []
 XCH = 4
 
 
@@ -65,26 +70,74 @@ def engine_plan(topo, src, dsts):
     lists = [topo.engines(src, d) for d in dsts]
     few = min(len(e) for e in lists)
     tight = [i for i in range(len(dsts)) if len(lists[i]) == few]
-    masks = [0] * len(dsts)
-    pool = list(lists[tight[0]])
-    used = 0
-    for n, i in enumerate(tight):
-        k = pow2(len(pool) // (len(tight) - n))
-        for e in pool[:k]:
-            masks[i] |= 1 << e
-        pool = pool[k:]
-        used |= masks[i]
+    calls = []
+    for n in range(0, len(tight), 2):
+        part, pool, call = tight[n:n + 2], list(lists[tight[n]]), []
+        for j, i in enumerate(part):
+            k = pow2(len(pool) // (len(part) - j))
+            call.append((i, sum(1 << e for e in pool[:k])))
+            pool = pool[k:]
+        calls.append(call)
+    used = sum(m for i, m in calls[0])
     for i in range(len(dsts)):
         if i not in tight:
             free = [e for e in lists[i] if not used >> e & 1]
-            for e in free[:pow2(len(free))]:
-                masks[i] |= 1 << e
-            used |= masks[i]
-    return masks
+            calls[0].append((i, sum(1 << e for e in free[:pow2(len(free))])))
+            used |= calls[0][-1][1]
+    return calls
 
 
 def bits(m):
     return bin(m).count("1")
+
+
+def touches(seen, q, reads, writes):
+    for kind, regs in ((0, reads), (1, writes)):
+        for b, lo, hi in regs:
+            psum = SCRATCH[b][0] == "psum"
+            for x in seen.get(b, []):
+                if psum and x[3] != q:
+                    if x[0] // 512 > (hi - 1) // 512 or (x[1] - 1) // 512 < lo // 512:
+                        continue
+                elif x[0] >= hi or x[1] <= lo or not (kind or x[2]):
+                    continue
+                yield x[4]
+
+
+def record(seen, q, reads, writes, tag):
+    for b, lo, hi in writes:
+        seen[b] = [x for x in seen.get(b, []) if not (x[0] >= lo and x[1] <= hi)] + [(lo, hi, 1, q, tag)]
+    for b, lo, hi in reads:
+        seen.setdefault(b, []).append((lo, hi, 0, q, tag))
+
+
+def plan_turns(held):
+    calls = range(len(held))
+    seen, first, then = {}, [], [[] for k in calls]
+    for k, (q, call, reads, writes, busy, late) in enumerate(held):
+        first.append(set(touches(seen, q, reads, writes)))
+        record(seen, q, reads, writes, k)
+        for j in first[k]:
+            then[j].append(k)
+
+    def lay(turn, needs, backward):
+        at = [0.0] * len(held)
+        taken = {}
+        for k in turn:
+            q, busy = held[k][0], held[k][4]
+            now = max([at[j] + held[j][4] + held[k if backward else j][5] + WAKE for j in needs[k]] + [held[k][5] * backward])
+            for lo, hi in taken.setdefault(q, []):
+                if now + busy <= lo:
+                    break
+                now = max(now, hi)
+            at[k] = now
+            taken[q] = sorted(taken[q] + [(now, now + busy)])
+        return at
+    at = lay(calls, first, 0)
+    for n in range(PASSES):
+        late = lay(sorted(calls, key=lambda k: -at[k] - held[k][4]), then, 1)
+        at = lay(sorted(calls, key=lambda k: -late[k] - held[k][4]), first, 0)
+    return sorted(calls, key=lambda k: at[k])
 
 
 def rank_program(g, core, T, topo):
@@ -108,61 +161,36 @@ def rank_program(g, core, T, topo):
 
     def order(q, reads, writes):
         need = {}
-        for kind, regs in ((0, reads), (1, writes)):
-            for b, lo, hi in regs:
-                psum = b in SCRATCH and SCRATCH[b][0] == "psum"
-                for l2, h2, w2, sem, val in log.get(b, []):
-                    if psum and sem != csem[q]:
-                        if l2 // 512 > (hi - 1) // 512 or (h2 - 1) // 512 < lo // 512:
-                            continue
-                    elif l2 >= hi or h2 <= lo or not (kind or w2):
-                        continue
-                    need[sem] = max(need.get(sem, 0), val)
+        for sem, val in touches(log, q, reads, writes):
+            need[sem] = max(need.get(sem, 0), val)
         for sem in need:
             wait(q, sem, need[sem])
 
-    def note(reads, writes, sem, val):
+    def note(q, reads, writes, sem, val):
         total[sem] = max(total.get(sem, 0), val)
-        for b, lo, hi in writes:
-            log[b] = [x for x in log.get(b, []) if not (x[0] >= lo and x[1] <= hi)] + [[lo, hi, 1, sem, val]]
-        for b, lo, hi in reads:
-            log.setdefault(b, []).append([lo, hi, 0, sem, val])
+        record(log, q, reads, writes, (sem, val))
 
-    def emit(call):
-        if held:
-            held[-1].append(call)
-        else:
-            call()
-
-    def weave(*chains):
-        runs = []
-        for chain in chains:
-            held.append([])
-            chain()
-            runs.append(held.pop())
-        for k in range(max(len(x) for x in runs)):
-            for x in runs:
-                if k < len(x):
-                    emit(x[k])
-
-    def op(q, fn, reads, writes):
+    def op(q, fn, reads, writes, busy=None):
         def call():
             order(q, reads, writes)
             ins = fn(Q[q])
             count[q] += 1
             ins.then_inc(T.sem[csem[q]], 1)
-            note(reads, writes, csem[q], count[q])
-        emit(call)
+            note(q, reads, writes, csem[q], count[q])
+        if busy is None:
+            narrow = q == "v" and all(SCRATCH[x[0]][2] in ("bfloat16", "uint16") for x in reads + writes)
+            busy = max(64, (writes[0][2] - writes[0][1]) * (2 if q == "g" else 0.5 if narrow else 1)) + (150 if q == "g" else 0)
+        held.append((q, call, reads, writes, busy * CYCLE, 0.0))
 
-    def dmas(q, pairs, reads, writes):
+    def dmas(q, pairs, reads, writes, late=LOCAL):
         def call():
             order(q, reads, writes)
             sem = "d%d" % nd[0]
             nd[0] += 1
             for out, in_ in pairs:
                 Q[q].dma_start(out, in_).then_inc(T.sem[sem], 16)
-            note(reads, writes, sem, 16 * len(pairs))
-        emit(call)
+            note(q, reads, writes, sem, 16 * len(pairs))
+        held.append((q, call, reads, writes, 0.06 * len(pairs), late))
 
     def dma(q, out, in_, reads, writes):
         dmas(q, [(out, in_)], reads, writes)
@@ -180,7 +208,8 @@ def rank_program(g, core, T, topo):
             op("v", lambda e: e.tensor_scalar(ap(out), ap(in0), s1, s2, o0, o1), [in0] + list(extra), [out])
 
     def tt(out, a, b, o):
-        op("v", lambda e: e.tensor_tensor(ap(out), ap(a), ap(b), o), [a, b], [out])
+        fast = SCRATCH[a[0]][2] == "bfloat16" or "psum" in SCRATCH[a[0]] + SCRATCH[b[0]]
+        op("v", lambda e: e.tensor_tensor(ap(out), ap(a), ap(b), o), [a, b], [out], max(64, (out[2] - out[1]) * (1 if fast else 2)))
 
     def cp(out, a):
         op("v", lambda e: e.tensor_copy(ap(out), ap(a)), [a], [out])
@@ -192,13 +221,13 @@ def rank_program(g, core, T, topo):
         return ap(win).indirect(ap(off))
 
     def ttg(out, win, off, b, o):
-        op("v", lambda e: e.tensor_tensor(ap(out), ind(win, off), ap(b), o), [win, off, b], [out])
+        op("v", lambda e: e.tensor_tensor(ap(out), ind(win, off), ap(b), o), [win, off, b], [out], 50 + GATHER * (out[2] - out[1]))
 
-    def act(out, a, func, bias=0.0, scale=1.0):
-        op("s", lambda e: e.activation(ap(out), ap(a), func, bias=bias, scale=scale), [a], [out])
+    def act(out, a, func, bias=0.0, scale=1.0, busy=None):
+        op("s", lambda e: e.activation(ap(out), ap(a), func, bias=bias, scale=scale), [a], [out], busy)
 
     def actg(out, win, off, bias=0.0):
-        op("s", lambda e: e.activation(ap(out), ind(win, off), F.Identity, bias=bias), [win, off], [out])
+        op("s", lambda e: e.activation(ap(out), ind(win, off), F.Identity, bias=bias), [win, off], [out], 65 + GATHER * (out[2] - out[1]))
 
     def iota(out, pattern, base, cm):
         op("g", lambda e: e.iota(ap(out), pattern, base, cm, allow_small_or_imprecise_dtypes=True), [], [out])
@@ -212,50 +241,47 @@ def rank_program(g, core, T, topo):
                 for k, (a, b) in enumerate(terms):
                     ins = e.matmul(ap(out), ap(a), ap(b), k == 0, k == len(terms) - 1)
             return ins
-        op("p", fn, [x for out, terms in groups for ab in terms for x in ab], [out for out, terms in groups])
+        op("p", fn, [x for out, terms in groups for ab in terms for x in ab], [out for out, terms in groups],
+           PE * sum(max(64, b[2] - b[1]) * (4 if SCRATCH[b[0]][2] == "float32" else 1) for out, terms in groups for a, b in terms))
 
     def wrap(ps, src, n, first):
         out = r(ps, 0, n // 16)
 
-        def head(e):
-            for k, (a, b) in enumerate(first):
-                ins = e.matmul(ap(out), ap(a), ap(b), k == 0, False)
-            return ins
-
         def fn(e):
+            for k, (a, b) in enumerate(first):
+                e.matmul(ap(out), ap(a), ap(b), k == 0, False)
             for i in range(16):
                 lo = 16 - i + 143 * (i & 1)
                 ins = e.matmul(ap(out), T.ST[:, lo:lo + 128], T[src][:, i:n:16], False, i == 15)
             return ins
-        op("p", head, [x for ab in first for x in ab], [out])
-        op("p", fn, [r("ST", 0, 288), r(src, 0, n)], [r(ps + "w", 0, 1)])
-        emit(lambda: note([], [out], "cp", count["p"]))
+        op("p", fn, [r("ST", 0, 288), r(src, 0, n)] + [x for ab in first for x in ab], [out], PE * 64 * (16 + len(first)))
 
-    def exchange(sign, srcs, land, land_lo, asem, lsem):
+    def exchange(sign, src, land, asem, lsem):
         def call():
             dsts = [T.cores[(rank + sign * (1 + h)) % N] for h in range(3)]
-            masks = engine_plan(topo, core, dsts)
-            order("g", srcs, [])
-            trs = []
-            for h in range(3):
-                rid, pid = topo.addr(dsts[h], core)
-                trs.append(RemoteDMATransfer(
-                    dst_ids=[DstId(rid=rid, pnc=pid)], dma_engine_mask=masks[h], remote_sem=T.sem[asem],
-                    srcs=[T[b][:, lo + 64 * h:lo + 64 * h + 64] for b, lo, hi in srcs],
-                    dsts=[T[land][:, land_lo + 64 * h:land_lo + 64 * h + 64]], alu_op=2 if len(srcs) > 1 else 0))
-            g.remote_dma_fused(trs, local_sem=T.sem[lsem])
-            note(srcs, [], lsem, sum(bits(x) for x in masks))
+            order("g", [src], [])
+            plan = engine_plan(topo, core, dsts)
+            for part in plan:
+                trs = []
+                for h, mask in part:
+                    rid, pid = topo.addr(dsts[h], core)
+                    trs.append(RemoteDMATransfer(
+                        dst_ids=[DstId(rid=rid, pnc=pid)], dma_engine_mask=mask, remote_sem=T.sem[asem],
+                        srcs=[T[src[0]][:, src[1] + 64 * h:src[1] + 64 * h + 64]],
+                        dsts=[T[land[0]][:, land[1] + 64 * h:land[1] + 64 * h + 64]], alu_op=0))
+                g.remote_dma_fused(trs, local_sem=T.sem[lsem])
+            note("g", [src], [], lsem, sum(bits(m) for part in plan for h, m in part))
             arrive = 0
             for h in range(3):
                 s = (rank - sign * (1 + h)) % N
                 sd = [T.cores[(s + sign * (1 + k)) % N] for k in range(3)]
-                arrive += bits(engine_plan(topo, T.cores[s], sd)[h])
-            note([], [r(land, land_lo, land_lo + ND)], asem, arrive)
-        emit(call)
+                arrive += sum(bits(m) for part in engine_plan(topo, T.cores[s], sd) for i, m in part if i == h)
+            note("g", [], [land], asem, arrive)
+        held.append(("g", call, [src], [land], 0.8, REMOTE))
 
     both, marks, vals = r("W", 0, WEND), r("W", 0, O + E), r("W", GAP, WEND)
     mdoor, vdoor = r("W", O, O + ND), r("W", TV, TV + ND)
-    eye, neg, eyeb, negb, neg2, eyeq, eyea, eyez = [r("ID", 128 * i, 128 * i + 128) for i in range(8)]
+    eye, neg, eyeb, negb, neg2, eyeq, eyea, eyez, eyeg = [r("ID", 128 * i, 128 * i + 128) for i in range(9)]
     zg, zd = r("pq", 128, 128 + ND), r("pcb", 128, 128 + ND)
 
     def nw(t):
@@ -264,42 +290,48 @@ def rank_program(g, core, T, topo):
     def thr(t, lo, hi):
         return r("QW", QB + 2 * NW * t + lo, QB + 2 * NW * t + hi)
 
-    dmas("y", [(T.kr[:, 16 * h:16 * h + 16], T.k0[h:8:2, 2 * ND:2 * ND + 512]) for h in range(2)], [], [r("kr", 0, 32)])
-    dma("s", T.kc[:, 192:384], T.k1[:], [], [r("kc", 192, 384)])
-    dma("s", ap(thr(0, 0, NR)), T.q[:], [], [thr(0, 0, NR)])
+    def block(b, k):
+        return r(b, ND * k, ND * k + ND)
+
+    def lists(t, k, m=M):
+        return r("P%d" % (t % 3), M * k, M * k + m)
+
+    def offsets(t, k, m=M):
+        return r("U%d" % (t & 1), M * k, M * k + m)
+
+    def back(t, m=M):
+        return r("Z%d" % (t & 1), 0, m)
+
     cw = E // XCH
+    dma("s", T.kc[:, 192:384], T.k1[:], [], [r("kc", 192, 384)])
+    dmas("y", [(T.kr[:, 16 * h:16 * h + 16], T.k0[h:8:2, 2 * ND:2 * ND + 512]) for h in range(2)], [], [r("kr", 0, 32)])
+    dma("s", ap(thr(0, 0, NR)), T.q[:], [], [thr(0, 0, NR)])
     for c in range(XCH):
-        dma("y" if c % 2 == 0 else "s", T.W[:, TV + c * cw:TV + (c + 1) * cw], T.x[:, c * cw:(c + 1) * cw], [],
-            [r("W", TV + c * cw, TV + (c + 1) * cw)])
+        dmas("y" if c % 2 else "s", [(T.W[:, TV + c * cw:TV + (c + 1) * cw], T.x[:, c * cw:(c + 1) * cw])], [],
+             [r("W", TV + c * cw, TV + (c + 1) * cw)], LOCAL + 0.3 * c)
     dma("y", T.kc[:, 0:192], T.k0[:], [], [r("kc", 0, 192)])
-    op("g", lambda e: e.iota(T.pi[:, 0:1], [[1, 1]], 0, 1), [], [r("pi", 0, 1)])
+    dma("y", T.Xn[:, 0:NR], T.x[:, 2 * ND:2 * ND + NR], [], [r("Xn", 0, NR)])
     iota(r("idf", 0, 128), [[1, 128]], 0, -1)
+    op("g", lambda e: e.iota(T.pi[:, 0:1], [[1, 1]], 0, 1), [], [r("pi", 0, 1)])
     iota(r("stf", 0, 288), [[1, 2], [1, 144]], -16, 0)
     iota(r("jraw"), [[16, M]], 0, 1)
-    fill(r("c85"), int(8.5 * BIG))
     fill(r("W", 0, O), 0)
+    fill(r("c85"), int(8.5 * BIG))
     iota(r("wa"), [[16, M]], 0, 0)
     iota(r("wc", 0, 9 * M), [[2 * NW, 9], [0, M]], QB + NW, 0)
-    fill(r("QW", 0, O), 0)
-    fill(r("c64"), O)
-    fill(r("W", GAP, TV), 0)
-    for t, lo in ((0, 0), (0, NW), (1, 0), (1, NW), (2, 0)):
+    for out, c in ((r("c64"), O), (r("QW", 0, O), 0), (r("QW", O + 2 * ND, O + cw), 0), (r("W", GAP, TV), 0)):
+        fill(out, c)
+    for t, lo in ((0, 0), (0, NW), (1, 0), (1, NW)):
         fill(thr(t, lo + NR, lo + NW), 100)
     fill(r("c128", 0, NW), -128)
-    fill(r("lv", 0, 64), 0)
-    fill(r("lw", 0, NW), 0)
-    iota(r("bdf", 0, 128), [[16, 8], [0, 16]], 0, 0)
 
     ts(eye, r("idf", 0, 128), 0.0, None, A.is_equal)
-    ms(r("KT", 0, O + E), 0.0)
-    ts(r("pi", 1, 2), r("pi", 0, 1), 112, None, A.bitwise_and)
-    ts(r("pi", 2, 3), r("pi", 0, 1), 14, None, A.bitwise_and)
-    ts(r("pi", 3, 4), r("pi", 0, 1), 15, None, A.bitwise_and)
-    ms(r("W", O + ND, O + 768), 0.0)
+    act(eyeb, eye, F.Silu, scale=B, busy=1500)
+    for k, c in enumerate((112, 14, 15)):
+        ts(r("pi", 1 + k, 2 + k), r("pi", 0, 1), c, None, A.bitwise_and)
     cp(r("pf", 0, 3), r("pi", 1, 4))
-    act(eyeb, eye, F.Silu, scale=B)
-    for m_, c in ((negb, -B), (neg, -1.0), (neg2, -2.0), (eyeq, -NW / B), (eyea, 16 * BIG), (eyez, 2176.0)):
-        act(m_, eye, F.Copy, scale=c)
+    ms(r("KT", 0, O + E), 0.0)
+    ms(r("W", O + ND, O + 768), 0.0)
 
     def link_table(f):
         lo = 192 * f
@@ -308,54 +340,71 @@ def rank_program(g, core, T, topo):
         dmas("y", [(T.KT[2 * f + h:128:16, O:O + E], T.kp[:, 384 * h + lo:384 * h + lo + 192]) for h in range(2)],
              [r("kp", lo, lo + 192), r("kp", 384 + lo, 576 + lo)], [r("KT", 0, O + E)])
 
-    def first_list():
-        ts(r("s3", 0, 32), r("kr", 0, 32), float(O), None, A.add)
-        op("v", lambda e: e.transpose(T.aa[:, 0:32], T.s3[:, 0:32]), [r("s3", 0, 32)], [r("aa", 0, 32)])
-        cp(r("cu", 0, 24), r("aa", 0, 24))
-
-    ts(r("ST", 0, 288), r("stf", 0, 288), T.pf[:, 0:1], -BIG, A.is_equal, A.mult, extra=[r("pf", 0, 1)])
-    ts(r("jj"), r("jraw"), T.pf[:, 0:1], None, A.subtract, extra=[r("pf", 0, 1)])
-    weave(lambda: link_table(1), first_list)
-    ts(thr(0, 0, NR), thr(0, 0, NR), 64.0, None, A.add)
+    link_table(1)
     ts(mdoor, vdoor, 64.0, None, A.add)
     for c in range(1, XCH):
         ts(r("W", O + c * cw, O + (c + 1) * cw), r("W", TV + c * cw, TV + (c + 1) * cw), 64.0, None, A.add)
-    for c in range(XCH):
-        act(r("QW", O + c * cw, O + (c + 1) * cw), r("W", TV + c * cw, TV + (c + 1) * cw), F.Identity, bias=62.0)
-        if c == 2:
-            act(r("Xn", 0, NR), r("W", TV + 2 * ND, TV + 2 * ND + NR), F.Copy)
+    ts(r("s3", 0, 32), r("kr", 0, 32), float(O), None, A.add)
+    op("v", lambda e: e.transpose(T.aa[:, 0:32], T.s3[:, 0:32]), [r("s3", 0, 32)], [r("aa", 0, 32)])
+    cp(r("cu", 0, 24), r("aa", 0, 24))
+    act(r("q2", 0, NR), thr(0, 0, NR), F.Identity, bias=62.0)
+    act(thr(0, NW, NW + NR), thr(0, 0, NR), F.Identity, bias=63.0)
+    ts(thr(0, 0, NR), thr(0, 0, NR), 64.0, None, A.add)
+    ts(r("ST", 0, 288), r("stf", 0, 288), T.pf[:, 0:1], -BIG, A.is_equal, A.mult, extra=[r("pf", 0, 1)])
+    for lo, hi in ((0, 2 * ND), (cw, 2 * cw), (2 * cw, 3 * cw), (3 * cw, E)):
+        act(r("QW", O + lo, O + hi), r("W", TV + lo, TV + hi), F.Identity, bias=62.0)
 
     def setup_lists():
-        ts(r("vv0", 0, 24), r("jj", 0, 24), float(2 * ND + O), None, A.add)
-        ts(r("vv0", 24, M), r("jj", 24, M), float(O - ND), None, A.add)
+        ts(r("jj"), r("jraw"), T.pf[:, 0:1], None, A.subtract, extra=[r("pf", 0, 1)])
         ts(r("wb"), r("jraw"), 0.0, T.pf[:, 2:3], A.mult, A.add, extra=[r("pf", 2, 3)])
-        for b in (2, 3):
-            ts(r("Z0", b * M, b * M + M), r("vv0"), float(GAP + 2 * TURN), None, A.add)
-        ts(r("LP", 24, M), r("vv0", 24, M), float(GAP), None, A.add)
-        ms(r("LP", M + 24, 2 * M), 0)
+        ts(r("P0", 0, 24), r("jj", 0, 24), float(2 * ND + O), None, A.add)
+        ts(r("P0", 24, M), r("jj", 24, M), float(O - ND), None, A.add)
+        for b in (3, 4):
+            ts(r("Z0", b * M, b * M + M), r("P0"), float(GAP + 2 * TURN), None, A.add)
+        ms(r("P1", 2 * M + 24, 3 * M), 0)
+        ts(r("P1", M + 24, 2 * M), r("P0", 24, M), float(GAP), None, A.add)
+        for k in range(2):
+            ts(r("pf", 4 + k, 5 + k), r("pf", 1, 2), 2.0 * k, -1.0 / BIG, A.is_equal, A.mult)
         ms(r("sg", 24, M), -1.0)
-        ts(r("pf", 4, 5), r("pf", 1, 2), 0.0, -1.0 / BIG, A.is_equal, A.mult)
-        ts(r("pf", 5, 6), r("pf", 1, 2), 2.0, -1.0 / BIG, A.is_equal, A.mult)
+        for m_, c in ((negb, -B), (neg, -1.0), (neg2, -2.0), (eyeq, -NW / B), (eyea, 16 * BIG), (eyez, 2176.0), (eyeg, -GAP / 2)):
+            act(m_, eye, F.Copy, scale=c)
 
-    def setup_links():
-        mm([(r("pe", 0, 384), [(eye, r("kp", 0, 384)), (eye, r("kp", 384, 768))])])
-        act(r("kf", 0, 384), r("pe", 0, 384), F.Identity, bias=float(O))
-        dmas("y", [(T.L[0:128:16, TV + TURN * f:TV + TURN * f + E], T.kf[:, 192 * f:192 * f + 192]) for f in range(2)],
-             [r("kf", 0, 384)], [r("L", 0, LW)])
+    def setup_second():
+        link_table(0)
+        ms(r("Z1", M, 2 * M), GAP)
+        ms(r("P2", 2 * M + 24, 3 * M), 0)
+        ts(r("P2", M + 24, 2 * M), r("P0", 24, M), float(GAP), None, A.add)
+        cp(r("Z1", 4 * M, 6 * M), r("Z0", 3 * M, 5 * M))
 
-    def setup_stack():
-        for b in (3, 4, 5, 6):
-            cp(r("Z1", b * M, b * M + M), r("Z0", 3 * M, 4 * M))
-        cp(r("Z0", 4 * M, 8 * M), r("Z1", 3 * M, 7 * M))
+    def setup_third():
+        cp(r("Z1", 6 * M, 8 * M), r("Z1", 4 * M, 6 * M))
+        cp(r("Z0", 5 * M, 9 * M), r("Z1", 4 * M, 8 * M))
+        fill(thr(2, NR, NW), 100)
+        iota(r("bdf", 0, 128), [[16, 8], [0, 16]], 0, 0)
+        for out, c in ((r("cz", 0, ND), 2176), (r("lv", 0, 64), 0), (r("lw", 0, NW), 0), (r("lw", 1024, 1024 + NW), 0)):
+            fill(out, c)
+        for k, c in enumerate((256.0, -256.0)):
+            ts(r("BD", 128 * k, 128 * k + 128), r("bdf", 0, 128), T.pf[:, 0:1], c, A.is_equal, A.mult, extra=[r("pf", 0, 1)])
+        act(r("g0", 0, ND), r("QW", O + ND, O + 2 * ND), F.Identity, bias=-62.0)
 
     def setup_guests():
         ts(r("s0", 0, 12), r("aa", 24, M), float(O + ND), None, A.is_ge)
-        ts(r("BD", 0, 128), r("bdf", 0, 128), T.pf[:, 0:1], 256.0, A.is_equal, A.mult, extra=[r("pf", 0, 1)])
-        tt(r("s1", 0, 12), r("s0", 0, 12), r("aa", 24, M), A.mult)
-        ts(r("BD", 128, 256), r("bdf", 0, 128), T.pf[:, 0:1], -256.0, A.is_equal, A.mult, extra=[r("pf", 0, 1)])
-        cp(r("gu", 0, 12), r("s1", 0, 12))
-        act(r("g0", 0, ND), r("QW", O + ND, O + 2 * ND), F.Identity, bias=-62.0)
+        tt(r("s3", 0, 12), r("s0", 0, 12), r("aa", 24, M), A.mult)
+        cp(r("gu", 0, 12), r("s3", 0, 12))
         actg(r("gt", 0, ND), r("QW", 0, O + E), r("gu", 0, 12), bias=-63.0)
+        tt(r("gb", 0, ND), r("gt", 0, ND), r("g0", 0, ND), A.max)
+
+    def setup_links():
+        mm([(r("pk", 128, 512), [(eye, r("kp", 0, 384)), (eye, r("kp", 384, 768))])])
+        act(r("kf", 0, 384), r("pk", 128, 512), F.Identity, bias=float(O))
+        dmas("y", [(T.L[0:128:16, O + TURN * f:O + TURN * f + E], T.kf[:, 192 * f:192 * f + 192]) for f in range(2)],
+             [r("kf", 0, 384)], [r("L", 0, LW)])
+
+    def setup_last():
+        for lo in range(0, O + E, 784):
+            iota(r("IOT", lo, lo + 784), [[1, 784]], lo - O, 0)
+        fill(r("m1", 0, NW), -1)
+        ts(r("idf", 0, 128), r("idf", 0, 128), 0.0, None, A.is_equal)
         cp(r("kd", 0, ND), r("kc", 0, ND))
         dmas("y", [(T.yk0[:, 0:ND], T.kd[0:128:16, :]), (T.yk1[:, 0:ND], T.kd[0:128:16, :])], [r("kd", 0, ND)], [])
 
@@ -367,30 +416,23 @@ def rank_program(g, core, T, topo):
         ttg(r("cmp", lo, hi), marks, r("cu", lo // 16, hi // 16), thr(t, lo, hi), A.is_ge)
 
     def countw(t):
-        m = nw(t) // 16
-        wrap("pcnt", "cmp", nw(t), [(eye, r("c85", 0, m))])
+        wrap("pcnt", "cmp", nw(t), [(eye, r("c85", 0, nw(t) // 16))])
 
     def before(t):
         f = t & 1
-        v, b, st = r("vv%d" % (t % 3)), r("bb%d" % (t % 3)), r("st%d" % f)
+        v, b, st, z = lists(t, 0), back(t), r("st%d" % f), "Z%d" % f
+        ts(b, r(z, 3 * M, 4 * M), TURN - 1, None, A.bitwise_and)
         if t > 0:
             if f == 0 or t == 1:
                 ts(st, v, float(O + ND), B, A.is_lt, A.mult)
             else:
                 ts(r("s0"), v, float(O + ND), B, A.is_lt, A.mult)
-        ts(b, r("Z%d" % f, 2 * M, 3 * M), TURN - 1, None, A.bitwise_and)
-        if f == 1 and t > 1:
-            tt(st, r("s0"), r("st0"), A.subtract)
-        ts(r("Z%d" % f), v, float(GAP + TURN * f), None, A.add)
-        if f == 1:
-            ts(r("eu"), b, float(-GAP), None, A.add)
-        if t > 0:
+                tt(st, r("s0"), r("st0"), A.subtract)
+            ts(r("EL%d" % f, 0, 3 * M), r(z, 0, 3 * M), float(-GAP), None, A.add)
             tt(r("s1"), b, st, A.subtract)
-        ts(r("Z%d" % f, M, 2 * M), v, float(GAP + TURN * f), None, A.add)
-        if t > 0:
             tt(r("bp"), r("s1"), v, A.max)
-        if t > 0 and f == 0:
-            cp(r("eu"), r("bp"))
+        for k in (1, 2):
+            ts(r(z, k * M, k * M + M), v, float(GAP + TURN * f), None, A.add)
         if t < 9:
             mm([(r("pq"), [(eye, r("wa")), (eye, r("wb")), (eye, r("wc", M * t, M * t + M))]
                  + ([(eyeq, st)] if t > 0 else []))])
@@ -403,21 +445,20 @@ def rank_program(g, core, T, topo):
         st, k = r("st%d" % f), depth(t)
         tt(r("mm", 0, m), r("aa", 0, m), r("pcnt", 0, m), A.max)
         act(r("sg", 0, m), r("pcnt", 0, m), F.Sign, scale=-1.0)
-        tt(r("LP", 0, m), r("mm", 0, m), r("bp" if t else "bb0", 0, m), A.min)
+        tt(lists(t + 1, 1, m), r("mm", 0, m), r("bp", 0, m) if t else back(0, m), A.min)
         if t < 9:
-            tt(r("LP", M, M + m), r("mm", 0, m), r("pq", 0, m), A.min)
-            ts(r("vv%d" % ((t + 1) % 3)), r("LP"), GAP - 1, None, A.bitwise_and)
-            cp(r("U", 0, 2 * M), r("LP", 0, 2 * M))
-            cp(r("vu%d" % (1 - f)), r("vv%d" % ((t + 1) % 3)))
+            tt(lists(t + 1, 2, m), r("mm", 0, m), r("pq", 0, m), A.min)
+            ts(lists(t + 1, 0), lists(t + 1, 1), GAP - 1, None, A.bitwise_and)
+            cp(offsets(t + 1, 0, 3 * M), lists(t + 1, 0, 3 * M))
         else:
-            cp(r("U"), r("LP"))
+            cp(offsets(t + 1, 1), lists(t + 1, 1))
         mm([(r("pm", M * j, M * j + M), [(eyeb, r("sg"))]) for j in range(k)]
            + [(r("pm", 256 + M * j, 256 + M * j + M), [(eye, st)]) for j in range(k) if t > 0]
            + [(r("pm", 512 + M * j, 512 + M * j + M), [(negb, r("sg"))] + ([(neg2, st)] if t > 0 else [])) for j in range(k)])
 
     def thresholds(t):
         n = nw(t)
-        ttg(thr(t + 1, 0, n), r("QW", 0, QB + 2 * NW * (t + 1)), r("U", M, M + n // 16), r("q2", 0, n), A.max)
+        ttg(thr(t + 1, 0, n), r("QW", 0, QB + 2 * NW * (t + 1)), offsets(t + 1, 2, n // 16), r("q2", 0, n), A.max)
 
     def lowered(t):
         n = nw(t)
@@ -426,23 +467,40 @@ def rank_program(g, core, T, topo):
 
     def kgather(t):
         f, n = t & 1, nw(t)
-        vu = r("vu%d" % f, 0, n // 16)
+        vu = offsets(t, 0, n // 16)
         op("s", lambda e: e.activation(T.Kg[:, 0:n], ind(r("KT", 0, O + E), vu), F.Copy, scale=T.pf[:, 4 + f:5 + f]),
-           [r("KT", 0, O + E), vu, r("pf", 4, 6)], [r("Kg", 0, n)])
+           [r("KT", 0, O + E), vu, r("pf", 4, 6)], [r("Kg", 0, n)], 65 + GATHER * n)
         wrap("pk", "Kg", n, [(eye, r("c64", 0, n // 16))])
 
     def scatter(t, a, b=None):
-        u = r("U", 0, nw(t) // 16)
+        u = offsets(t + 1, 1, nw(t) // 16)
         if b is None:
-            op("v", lambda e: e.tensor_copy(ind(both, u), ap(a)), [u, a], [both])
+            op("v", lambda e: e.tensor_copy(ind(both, u), ap(a)), [u, a], [both], 50 + SCATTER * nw(t))
         else:
-            op("v", lambda e: e.tensor_tensor(ind(both, u), ap(a), ap(b), A.add), [u, a, b], [both])
+            op("v", lambda e: e.tensor_tensor(ind(both, u), ap(a), ap(b), A.add), [u, a, b], [both], 50 + SCATTER * nw(t))
 
     def here(t):
-        actg(r("G", 0, nw(t)), vals, r("vu%d" % (t & 1), 0, nw(t) // 16), bias=-1.0)
+        h, u = nw(t) // (1 + (t & 1)), offsets(t, 0)
+        for lo in range(0, nw(t), h):
+            actg(r("G", lo, lo + h), vals, r(u[0], lo // 16, (lo + h) // 16), bias=-1.0)
 
-    def differ(n, a, b):
-        mm([(r("pe", lo, hi), [(eye, r(a, lo, hi)), (neg, r(b, lo, hi))]) for lo, hi in ((0, min(n, 512)), (512, n)) if hi > lo])
+    def behind(t, bias=0.0):
+        actg(r("Ee", 0, nw(t)), vals, r("EL%d" % (t & 1), 0, nw(t) // 16), bias=bias)
+
+    def differ(n, a, b, early):
+        h = n // 2
+        for lo, p0 in ((0, 0), (h, 512)):
+            out = r("pe", p0, p0 + h)
+            terms = [(eye, r(a, lo, lo + h)), (neg, r(b, lo, lo + h))]
+            if early == b:
+                terms.reverse()
+            for k, (x, y) in enumerate(terms):
+                op("p", lambda e, x=x, y=y, k=k, out=out: e.matmul(ap(out), ap(x), ap(y), k == 0, k == 1),
+                   [x, y] + [out] * k, [out], PE * h)
+
+    def from_differ(out, n, func, **kw):
+        for lo, p0 in ((0, 0), (n // 2, 512)):
+            act(r(out, lo, lo + n // 2), r("pe", p0, p0 + n // 2), func, **kw)
 
     def countb(t):
         m = nw(t) // 16
@@ -451,23 +509,22 @@ def rank_program(g, core, T, topo):
     def stack(t):
         f = t & 1
         zo, zn, zw = "Z%d" % f, "Z%d" % (1 - f), M * depth(t)
-        tt(r("zm", 0, zw), r(zo, 2 * M, 2 * M + zw), r("pm", 512, 512 + zw), A.min)
-        tt(r("pm", 0, zw), r(zo, 0, zw), r("pm", 0, zw), A.min)
+        tt(r("zm", 0, zw), r(zo, 3 * M, 3 * M + zw), r("pm", 512, 512 + zw), A.min)
+        tt(r("pm", 0, zw), r(zo, M, M + zw), r("pm", 0, zw), A.min)
         if t > 0:
-            tt(r("zb", 0, zw), r(zo, M, M + zw), r("pm", 256, 256 + zw), A.min)
+            tt(r("zb", 0, zw), r(zo, 2 * M, 2 * M + zw), r("pm", 256, 256 + zw), A.min)
             tt(r("pm", 0, zw), r("zm", 0, zw), r("pm", 0, zw), A.max)
-            tt(r(zn, M, M + zw), r("zb", 0, zw), r("pm", 0, zw), A.max)
+            tt(r(zn, 2 * M, 2 * M + zw), r("zb", 0, zw), r("pm", 0, zw), A.max)
         else:
-            tt(r(zn, M, M + zw), r("zm", 0, zw), r("pm", 0, zw), A.max)
-        cp(r("lo%d" % f), r(zn, M, 2 * M))
+            tt(r(zn, 2 * M, 2 * M + zw), r("zm", 0, zw), r("pm", 0, zw), A.max)
 
     def link_values(t):
         f, m = t & 1, nw(t) // 16
         if t == 0:
-            cp(r("lv", 0, m), r("bb0", 0, m))
+            cp(r("lv", 0, m), back(0, m))
         else:
-            tt(r("s2", 0, m), r("vv%d" % (t % 3), 0, m), r("pcb", 0, m), A.max)
-            tt(r("lv", 0, m), r("s2", 0, m), r("bb%d" % (t % 3), 0, m), A.min)
+            tt(r("s2", 0, m), lists(t, 0, m), r("pcb", 0, m), A.max)
+            tt(r("lv", 0, m), r("s2", 0, m), back(t, m), A.min)
         nb = (m + 31) // 32
         lt = r("lt", 64 * f, 64 * f + 32 * nb)
         op("v", lambda e: e.transpose(ap(lt), T.lv[:, 0:32 * nb]), [r("lv", 0, 64)], [lt])
@@ -475,171 +532,147 @@ def rank_program(g, core, T, topo):
                     T.lt[:, 64 * f + 32 * b + 16 * h:64 * f + 32 * b + 16 * h + 16]) for b in range(nb) for h in range(2)],
              [lt], [r("lw", 1024 * f, 1024 * f + 1024)])
 
-    def link_write(t):
-        f, n = t & 1, nw(t)
-        lo, lw = r("lo%d" % f, 0, n // 16), r("lw", 1024 * f, 1024 * f + n)
-        op("s", lambda e: e.activation(ind(r("L", 0, LW), lo), ap(lw), F.Silu), [lo, lw], [r("L", 0, LW)])
-
-    def exact_write(t):
-        tt(r("s2"), r("vv%d" % (t % 3)), r("pcb"), A.max)
-        tt(r("li"), r("s2"), r("bb%d" % (t % 3)), A.min)
+    def last_values(t):
+        tt(r("s2"), lists(t, 0), r("pcb"), A.max)
+        tt(r("li"), r("s2"), back(t), A.min)
         ts(r("li"), r("li"), GAP - 1, None, A.bitwise_and)
         cp(r("lu"), r("li"))
         actg(r("lx", NW * (t & 1), NW * (t & 1) + NW), r("IOT", 0, O + E), r("lu"))
 
-    def exact_scatter(t):
-        lo, lx = r("lo%d" % (t & 1)), r("lx", NW * (t & 1), NW * (t & 1) + NW)
-        op("v", lambda e: e.tensor_copy(ind(r("L", 0, LW), lo), ap(lx)), [lo, lx], [r("L", 0, LW)])
+    def link_write(t):
+        n = nw(t)
+        lo = r("EL%d" % (1 - (t & 1)), 2 * M, 2 * M + n // 16)
+        if t < 8:
+            lw = r("lw", 1024 * (t & 1), 1024 * (t & 1) + n)
+            op("s", lambda e: e.activation(ind(r("L", 0, LW), lo), ap(lw), F.Silu), [lo, lw], [r("L", 0, LW)], 65 + SCATTER * n)
+        else:
+            lw = r("lx", NW * (t & 1), NW * (t & 1) + NW)
+            op("v", lambda e: e.tensor_copy(ind(r("L", 0, LW), lo), ap(lw)), [lo, lw], [r("L", 0, LW)], 50 + SCATTER * n)
 
     def link_rows(f):
-        return T.L[0:128:16, TV + TURN * f + ND:TV + TURN * f + E]
+        return T.L[0:128:16, O + TURN * f + ND:O + TURN * f + E]
 
-    def guests_retreat():
-        mm([(zg, [(eyez, r("se", 0, ND)), (r("BD", 128, 256), r("cmp", NR, NW))])])
+    def round_links():
+        cc, cs, ps = r("cc", 0, 2 * CW), r("cs", 0, 2 * CW), r("pk", 128, 128 + 2 * CW)
+        dmas("y", [(T.cc[:, CW * f:CW * f + CW], link_rows(f)) for f in range(2)], [r("L", 0, LW)], [cc])
+        act(cs, cc, F.Sign, bias=-4000.0)
+        mm([(ps, [(r("idf", 0, 128), cc), (eyeg, cs)])])
+        act(cc, ps, F.Identity, bias=MAGIC)
+        act(cc, cc, F.Identity, bias=-MAGIC - GAP // 2 - O)
+        dmas("y", [(link_rows(f), T.cc[:, CW * f:CW * f + CW]) for f in range(2)], [cc], [r("L", 0, LW)])
 
     def guests_back(ph):
-        u2, snd = r("u2", ND * (ph - 1), ND * ph), r("snd", ND * (ph - 1), ND * ph)
-        tt(u2, r("gb", 0, ND), zg, A.min)
-        if not FOLD:
-            tt(snd, u2, r("g0", 0, ND), A.max)
-        exchange(-1, [u2, r("g0", 0, ND)] if FOLD else [snd], "rb", ND * (ph - 1), "ba%d" % (ph - 1), "bl%d" % (ph - 1))
-
-    def waiting(ph):
-        return r("mk", ND * (ph & 1), ND * (ph & 1) + ND)
+        mm([(zg, [(eyez, r("se", 0, ND)), (r("BD", 128, 256), r("cmp", NR, NW))])])
+        tt(r("u2", 0, ND), r("gb", 0, ND), zg, A.min)
+        tt(block("snd", ph - 1), r("u2", 0, ND), r("g0", 0, ND), A.max)
+        exchange(-1, block("snd", ph - 1), block("rb", ph - 1), "ba%d" % (ph - 1), "bl%d" % (ph - 1))
 
     def doors_take(ph):
-        tt(r("t1", 0, ND), r("rb", ND * (ph - 1), ND * ph), waiting(ph - 1), A.min)
+        tt(r("t1", 0, ND), block("rb", ph - 1), block("mk", (ph - 1) & 1), A.min)
         tt(vdoor, r("vd", 0, ND), r("t1", 0, ND), A.max)
 
     def doors_clear(ph):
-        mm([(zd, [(eye, vdoor), (neg, waiting(ph))])])
+        mm([(zd, [(eye, vdoor), (neg, block("mk", ph & 1))])])
         act(r("vd", 0, ND), zd, F.Relu)
 
     compare(0, 0, NR)
     countw(0)
     setup_lists()
     before(0)
-    lowered(0)
     for ph in range(5):
         t = 2 * ph
         n = nw(t)
-        wide = [r(b, 0, n) for b in ("Xn", "Ee", "Rv", "cmpb", "pe")]
-        if ph > 0:
-            here(t)
-            if EVEN_ON_SCALAR:
-                actg(wide[1], both, r("eu"))
-                differ(n, "G", "Ee")
-            tt(thr(t, NR, NW), thr(t, NR, NW), r("rp", 0, ND), A.min)
-            compare(t, NR, NW)
-            countw(t)
-            mm([(zg, [(neg, r("cz", 0, ND)), (r("BD", 0, 128), r("cmp", NR, NW))])])
-            if EVEN_ON_SCALAR:
-                act(wide[2], wide[4], F.Relu)
-            lowered(t)
-            link_values(t - 1)
-            if not EVEN_ON_SCALAR:
-                ttg(wide[0], both, r("eu"), r("G", 0, n), A.max)
-                differ(n, "Xn", "G")
         decide(t)
+        scatter(t, r("Xn", 0, n))
         kgather(t + 1)
-        if ph > 0 and EVEN_ON_SCALAR:
-            scatter(t, wide[1], wide[2])
-        else:
-            scatter(t, wide[0])
         thresholds(t)
-        if ph == 0:
-            link_table(0)
-            setup_stack()
-        else:
-            act(r("se", 0, ND), zg, F.Sign)
-            act(wide[3], wide[4], F.Sign, bias=1.5, scale=1.0 if EVEN_ON_SCALAR else -1.0)
-            if ph == 1:
-                tt(r("gb", 0, ND), r("gt", 0, ND), r("g0", 0, ND), A.max)
-            doors_clear(ph - 1)
         t += 1
+        named(t)
+        if ph > 0:
+            act(r("se", 0, ND), zg, F.Sign)
+            compare(t, NR, NW)
+            guests_back(ph)
+        compare(t, 0, NR)
+        countw(t)
+        if ph == 0:
+            setup_second()
+        stack(t - 1)
+        if ph > 0:
+            link_write(t - 3)
+        before(t)
+        if ph > 0:
+            from_differ("cmpb", n, F.Sign, bias=1.5, scale=-1.0)
+            countb(t - 1)
+            doors_clear(ph - 1)
         if ph == 4:
             break
-        named(t)
-        compare(t, 0, n)
-        if ph > 0:
-            guests_retreat()
-        countw(t)
         lowered(t)
-        if ph > 0:
-            link_write(t - 2)
-            countb(t - 1)
-            weave(lambda: stack(t - 1), lambda: guests_back(ph))
-        else:
-            stack(t - 1)
-        before(t)
-        actg(wide[1], vals, r("eu", 0, n // 16))
-        if ph == 0:
-            here(t)
+        behind(t)
         decide(t)
         thresholds(t)
-        kgather(t + 1)
         scatter(t, thr(t + 1, 0, n), r("c128", 0, n))
-        exchange(1, [mdoor], "rf", ND * ph, "fa%d" % ph, "fl%d" % ph)
-        if ph == 0:
-            fill(r("cz", 0, ND), 2176)
-            fill(r("W", O + E, GAP), 0)
-            fill(r("lw", 1024, 1024 + NW), 0)
-            setup_links()
-        elif ph < 3:
-            lo = (O + E) // 2 * (ph - 1)
-            iota(r("IOT", lo, lo + (O + E) // 2), [[1, (O + E) // 2]], lo - O, 0)
-        else:
-            fill(r("c128", 0, NW), -1)
+        act(block("rp", ph), mdoor, F.Identity, bias=128.0)
+        exchange(1, block("rp", ph), block("rf", ph), "fa%d" % ph, "fl%d" % ph)
         if ph > 0:
-            weave(lambda: doors_take(ph), lambda: link_values(t - 1))
-            here(t)
-        else:
-            link_values(t - 1)
-        differ(n, "G", "Ee")
-        act(waiting(ph), mdoor, F.Relu, bias=-20.0, scale=-1.0)
-        act(wide[2], wide[4], F.Relu)
-        act(wide[3], wide[4], F.Sign, bias=1.5)
-        countb(t)
+            doors_take(ph)
+        here(t)
+        differ(n, "G", "Ee", "Ee")
+        from_differ("Rv", n, F.Relu)
+        scatter(t, r("Ee", 0, n), r("Rv", 0, n))
+        from_differ("cmpb", n, F.Sign, bias=1.5)
+        kgather(t + 1)
+        if ph == 0:
+            setup_third()
         stack(t)
-        named(t + 1)
-        compare(t + 1, 0, NR)
+        if ph > 0:
+            link_write(t - 2)
+        link_values(t - 1)
+        t += 1
+        before(t)
+        here(t)
+        named(t)
+        compare(t, 0, NR)
+        tt(thr(t, NR, NW), thr(t, NR, NW), block("rf", ph), A.min)
+        compare(t, NR, NW)
+        countw(t)
+        ttg(r("Xn", 0, NW), vals, r("EL0"), r("G", 0, NW), A.max)
+        differ(NW, "Xn", "G", "G")
+        lowered(t)
+        mm([(zg, [(neg, r("cz", 0, ND)), (r("BD", 0, 128), r("cmp", NR, NW))])])
+        act(block("mk", ph & 1), block("rp", ph), F.Relu, bias=108.0, scale=-1.0)
+        countb(t - 1)
+        link_values(t - 1)
         if ph == 0:
             setup_guests()
-        before(t + 1)
-        scatter(t, wide[1], wide[2])
-        act(r("rp", 0, ND), r("rf", ND * ph, ND * ph + ND), F.Identity, bias=128.0)
-        link_write(t - 1)
+            setup_links()
+        if ph == 2:
+            setup_last()
 
-    link_write(7)
-    dmas("y", [(T.cc[:, CW * f:CW * f + CW], link_rows(f)) for f in range(2)], [r("L", 0, LW)], [r("cc", 0, 2 * CW)])
-    named(9)
-    compare(9, NR, NW)
-    guests_retreat()
-    compare(9, 0, NR)
-    countw(9)
-    countb(8)
-    weave(lambda: guests_back(4), lambda: stack(8))
-    before(9)
-    actg(r("Ee", 0, NW), vals, r("eu"), bias=1.0)
+    behind(9, 1.0)
+    last_values(8)
     decide(9)
-    weave(lambda: exact_write(8), lambda: stack(9))
-    cp(r("ci", 0, 2 * CW), r("cc", 0, 2 * CW))
-    ts(r("ci", 0, 2 * CW), r("ci", 0, 2 * CW), GAP - 1, None, A.bitwise_and)
-    ts(r("cc", 0, 2 * CW), r("ci", 0, 2 * CW), float(-O), None, A.add)
-    dmas("y", [(link_rows(f), T.cc[:, CW * f:CW * f + CW]) for f in range(2)], [r("cc", 0, 2 * CW)], [r("L", 0, LW)])
+    link_write(7)
+    round_links()
     doors_take(4)
+    ttg(r("Xn", 0, NW), vals, offsets(9, 0), r("Ee", 0, NW), A.max)
     here(9)
-    ttg(r("Xn", 0, NW), vals, r("vu1"), r("Ee", 0, NW), A.max)
-    differ(NW, "G", "Ee")
-    act(r("cmpb", 0, NW), r("pe", 0, NW), F.Sign, bias=2.5)
-    countb(9)
-    scatter(9, r("Xn", 0, NW), r("c128", 0, NW))
+    scatter(9, r("Xn", 0, NW), r("m1", 0, NW))
     for c in range(2):
-        dma("y" if c else "s", T.yx[:, 1536 * c:1536 * c + 1536], T.W[:, TV + 1536 * c:TV + 1536 * c + 1536], [vals], [])
-    exact_write(9)
-    exact_scatter(8)
-    exact_scatter(9)
+        dmas("y" if c else "s", [(T.yx[:, 1536 * c:1536 * c + 1536], T.W[:, TV + 1536 * c:TV + 1536 * c + 1536])], [vals], [], 5.5)
+    differ(NW, "G", "Ee", "Ee")
+    from_differ("cmpb", NW, F.Sign, bias=2.5)
+    countb(9)
+    last_values(9)
+    link_write(8)
+    stack(9)
+    ts(r("EL0", 2 * M, 3 * M), r("Z0", 2 * M, 3 * M), float(-GAP), None, A.add)
+    link_write(9)
     dma("y", T.yk0[:, ND:E], link_rows(0), [r("L", 0, LW)], [])
     dma("s", T.yk1[:, ND:E], link_rows(1), [r("L", 0, LW)], [])
+
+    if not TURNS:
+        TURNS.extend(plan_turns(held))
+    for k in TURNS:
+        held[k][1]()
     for sem in total:
         wait("y", sem, total[sem])

from concourse.bass import DstId, RemoteDMATransfer
from concourse.mybir import AluOpType as A, ActivationFunctionType as F

E, ND, NR, NW, M = 3072, 192, 384, 576, 36
O = 64
GAP = 4096
TV, WEND = GAP + O, GAP + O + E
TURN = 8192
LW = 2 * TURN + O + 2 * ND + NR
QB = O + E
BIG, B = 65536.0, 32768.0
CW = (E - ND) // 16
MAGIC = 12582912.0
CYCLE, PE, GATHER, WAKE = 0.00095, 0.72, 1.5, 0.08
SCATTER = 3.0
REMOTE = 2.4
LOCAL = 1.8
PASSES = 2


def sb(n, dtype="float32"):
    return ("sbuf", [128, n], dtype)


def bf(n):
    return sb(n, "bfloat16")


def i32(n):
    return sb(n, "int32")


def u16(n):
    return sb(n, "uint16")


SCRATCH = {
    "W": bf(WEND), "QW": bf(QB + 20 * NW), "KT": bf(O + E), "L": sb(LW), "IOT": sb(O + E), "ST": bf(288),
    "ID": bf(9 * 128), "BD": bf(256), "stf": sb(288), "idf": sb(128), "bdf": sb(128), "kr": i32(32), "kc": i32(384),
    "kp": bf(768), "kf": sb(384), "kd": sb(ND), "cc": sb(384), "cs": bf(384), "pi": i32(8), "pf": sb(8),
    "jraw": sb(M), "jj": sb(M), "wa": bf(M), "wb": bf(M), "wc": bf(9 * M), "c64": bf(M), "c85": bf(M), "cz": bf(ND),
    "c128": bf(NW), "m1": bf(NW),
    "q2": bf(NW), "cmp": bf(NW), "G": bf(NW), "Ee": bf(NW), "Rv": bf(NW), "Xn": bf(NW), "Kg": bf(NW),
    "cmpb": bf(NW), "lw": sb(2048), "lx": sb(2 * NW), "lv": sb(64), "lt": sb(128), "li": i32(M), "lu": u16(M),
    "g0": bf(ND), "gt": bf(ND), "gb": bf(ND), "se": bf(ND), "u2": bf(ND), "mk": bf(2 * ND), "t1": bf(ND),
    "rp": bf(4 * ND), "vd": bf(ND), "snd": bf(4 * ND), "rf": bf(4 * ND), "rb": bf(4 * ND),
    "aa": sb(M), "mm": sb(M), "P0": i32(3 * M), "P1": i32(3 * M), "P2": i32(3 * M), "U0": u16(3 * M), "U1": u16(3 * M),
    "cu": u16(M), "EL0": u16(3 * M), "EL1": u16(3 * M), "gu": u16(12), "st0": bf(M), "st1": bf(M), "sg": bf(M),
    "s0": sb(M), "s1": sb(M), "s2": sb(M), "s3": sb(M), "bp": sb(M),
    "Z0": i32(9 * M), "Z1": i32(9 * M), "zm": sb(6 * M), "zb": sb(6 * M),
    "pcnt": ("psum", [128, 512], "float32"), "pk": ("psum", [128, 512], "float32"),
    "pe": ("psum", [128, 1024], "float32"), "pcb": ("psum", [128, 512], "float32"),
    "pm": ("psum", [128, 1024], "float32"), "pq": ("psum", [128, 512], "float32"),
}
NDMA = 32
SEMAPHORES = (["cv", "cs", "cp", "cg"] + ["d%d" % i for i in range(NDMA)] + ["fa%d" % i for i in range(4)]
              + ["ba%d" % i for i in range(4)] + ["fl%d" % i for i in range(4)] + ["bl%d" % i for i in range(4)])
TURNS = []
XCH = 4


def pow2(n):
    k = 1
    while 2 * k <= n:
        k *= 2
    return k


def engine_plan(topo, src, dsts):
    lists = [topo.engines(src, d) for d in dsts]
    few = min(len(e) for e in lists)
    tight = [i for i in range(len(dsts)) if len(lists[i]) == few]
    calls = []
    for n in range(0, len(tight), 2):
        part, pool, call = tight[n:n + 2], list(lists[tight[n]]), []
        for j, i in enumerate(part):
            k = pow2(len(pool) // (len(part) - j))
            call.append((i, sum(1 << e for e in pool[:k])))
            pool = pool[k:]
        calls.append(call)
    used = sum(m for i, m in calls[0])
    for i in range(len(dsts)):
        if i not in tight:
            free = [e for e in lists[i] if not used >> e & 1]
            calls[0].append((i, sum(1 << e for e in free[:pow2(len(free))])))
            used |= calls[0][-1][1]
    return calls


def bits(m):
    return bin(m).count("1")


def touches(seen, q, reads, writes):
    for kind, regs in ((0, reads), (1, writes)):
        for b, lo, hi in regs:
            psum = SCRATCH[b][0] == "psum"
            for x in seen.get(b, []):
                if psum and x[3] != q:
                    if x[0] // 512 > (hi - 1) // 512 or (x[1] - 1) // 512 < lo // 512:
                        continue
                elif x[0] >= hi or x[1] <= lo or not (kind or x[2]):
                    continue
                yield x[4]


def record(seen, q, reads, writes, tag):
    for b, lo, hi in writes:
        seen[b] = [x for x in seen.get(b, []) if not (x[0] >= lo and x[1] <= hi)] + [(lo, hi, 1, q, tag)]
    for b, lo, hi in reads:
        seen.setdefault(b, []).append((lo, hi, 0, q, tag))


def plan_turns(held):
    calls = range(len(held))
    seen, first, then = {}, [], [[] for k in calls]
    for k, (q, call, reads, writes, busy, late) in enumerate(held):
        first.append(set(touches(seen, q, reads, writes)))
        record(seen, q, reads, writes, k)
        for j in first[k]:
            then[j].append(k)

    def lay(turn, needs, backward):
        at = [0.0] * len(held)
        taken = {}
        for k in turn:
            q, busy = held[k][0], held[k][4]
            now = max([at[j] + held[j][4] + held[k if backward else j][5] + WAKE for j in needs[k]] + [held[k][5] * backward])
            for lo, hi in taken.setdefault(q, []):
                if now + busy <= lo:
                    break
                now = max(now, hi)
            at[k] = now
            taken[q] = sorted(taken[q] + [(now, now + busy)])
        return at
    at = lay(calls, first, 0)
    for n in range(PASSES):
        late = lay(sorted(calls, key=lambda k: -at[k] - held[k][4]), then, 1)
        at = lay(sorted(calls, key=lambda k: -late[k] - held[k][4]), first, 0)
    return sorted(calls, key=lambda k: at[k])


def rank_program(g, core, T, topo):
    rank = T.rank_of(core)
    if rank is None:
        return
    N = len(T.cores)
    Q = {"v": g.vector, "s": g.scalar, "p": g.tensor, "g": g, "y": g.sync}
    csem = {"v": "cv", "s": "cs", "p": "cp", "g": "cg"}
    count = {"v": 0, "s": 0, "p": 0, "g": 0}
    waited = {q: {} for q in Q}
    log = {}
    total = {}
    nd = [0]
    held = []

    def wait(q, sem, val):
        if waited[q].get(sem, 0) < val:
            Q[q].wait_ge(T.sem[sem], val)
            waited[q][sem] = val

    def order(q, reads, writes):
        need = {}
        for sem, val in touches(log, q, reads, writes):
            need[sem] = max(need.get(sem, 0), val)
        for sem in need:
            wait(q, sem, need[sem])

    def note(q, reads, writes, sem, val):
        total[sem] = max(total.get(sem, 0), val)
        record(log, q, reads, writes, (sem, val))

    def op(q, fn, reads, writes, busy=None):
        def call():
            order(q, reads, writes)
            ins = fn(Q[q])
            count[q] += 1
            ins.then_inc(T.sem[csem[q]], 1)
            note(q, reads, writes, csem[q], count[q])
        if busy is None:
            narrow = q == "v" and all(SCRATCH[x[0]][2] in ("bfloat16", "uint16") for x in reads + writes)
            busy = max(64, (writes[0][2] - writes[0][1]) * (2 if q == "g" else 0.5 if narrow else 1)) + (150 if q == "g" else 0)
        held.append((q, call, reads, writes, busy * CYCLE, 0.0))

    def dmas(q, pairs, reads, writes, late=LOCAL):
        def call():
            order(q, reads, writes)
            sem = "d%d" % nd[0]
            nd[0] += 1
            for out, in_ in pairs:
                Q[q].dma_start(out, in_).then_inc(T.sem[sem], 16)
            note(q, reads, writes, sem, 16 * len(pairs))
        held.append((q, call, reads, writes, 0.06 * len(pairs), late))

    def dma(q, out, in_, reads, writes):
        dmas(q, [(out, in_)], reads, writes)

    def r(b, lo=0, hi=M):
        return (b, lo, hi)

    def ap(x):
        return T[x[0]][:, x[1]:x[2]]

    def ts(out, in0, s1, s2, o0, o1=None, extra=()):
        if o1 is None:
            op("v", lambda e: e.tensor_scalar(ap(out), ap(in0), s1, None, o0), [in0] + list(extra), [out])
        else:
            op("v", lambda e: e.tensor_scalar(ap(out), ap(in0), s1, s2, o0, o1), [in0] + list(extra), [out])

    def tt(out, a, b, o):
        fast = SCRATCH[a[0]][2] == "bfloat16" or "psum" in SCRATCH[a[0]] + SCRATCH[b[0]]
        op("v", lambda e: e.tensor_tensor(ap(out), ap(a), ap(b), o), [a, b], [out], max(64, (out[2] - out[1]) * (1 if fast else 2)))

    def cp(out, a):
        op("v", lambda e: e.tensor_copy(ap(out), ap(a)), [a], [out])

    def ms(out, c):
        op("v", lambda e: e.memset(ap(out), c), [], [out])

    def ind(win, off):
        return ap(win).indirect(ap(off))

    def ttg(out, win, off, b, o):
        op("v", lambda e: e.tensor_tensor(ap(out), ind(win, off), ap(b), o), [win, off, b], [out], 50 + GATHER * (out[2] - out[1]))

    def act(out, a, func, bias=0.0, scale=1.0, busy=None):
        op("s", lambda e: e.activation(ap(out), ap(a), func, bias=bias, scale=scale), [a], [out], busy)

    def actg(out, win, off, bias=0.0):
        op("s", lambda e: e.activation(ap(out), ind(win, off), F.Identity, bias=bias), [win, off], [out], 65 + GATHER * (out[2] - out[1]))

    def iota(out, pattern, base, cm):
        op("g", lambda e: e.iota(ap(out), pattern, base, cm, allow_small_or_imprecise_dtypes=True), [], [out])

    def fill(out, c):
        iota(out, [[0, out[2] - out[1]]], c, 0)

    def mm(groups):
        def fn(e):
            for out, terms in groups:
                for k, (a, b) in enumerate(terms):
                    ins = e.matmul(ap(out), ap(a), ap(b), k == 0, k == len(terms) - 1)
            return ins
        op("p", fn, [x for out, terms in groups for ab in terms for x in ab], [out for out, terms in groups],
           PE * sum(max(64, b[2] - b[1]) * (4 if SCRATCH[b[0]][2] == "float32" else 1) for out, terms in groups for a, b in terms))

    def wrap(ps, src, n, first):
        out = r(ps, 0, n // 16)

        def fn(e):
            for k, (a, b) in enumerate(first):
                e.matmul(ap(out), ap(a), ap(b), k == 0, False)
            for i in range(16):
                lo = 16 - i + 143 * (i & 1)
                ins = e.matmul(ap(out), T.ST[:, lo:lo + 128], T[src][:, i:n:16], False, i == 15)
            return ins
        op("p", fn, [r("ST", 0, 288), r(src, 0, n)] + [x for ab in first for x in ab], [out], PE * 64 * (16 + len(first)))

    def exchange(sign, src, land, asem, lsem):
        def call():
            dsts = [T.cores[(rank + sign * (1 + h)) % N] for h in range(3)]
            order("g", [src], [])
            plan = engine_plan(topo, core, dsts)
            for part in plan:
                trs = []
                for h, mask in part:
                    rid, pid = topo.addr(dsts[h], core)
                    trs.append(RemoteDMATransfer(
                        dst_ids=[DstId(rid=rid, pnc=pid)], dma_engine_mask=mask, remote_sem=T.sem[asem],
                        srcs=[T[src[0]][:, src[1] + 64 * h:src[1] + 64 * h + 64]],
                        dsts=[T[land[0]][:, land[1] + 64 * h:land[1] + 64 * h + 64]], alu_op=0))
                g.remote_dma_fused(trs, local_sem=T.sem[lsem])
            note("g", [src], [], lsem, sum(bits(m) for part in plan for h, m in part))
            arrive = 0
            for h in range(3):
                s = (rank - sign * (1 + h)) % N
                sd = [T.cores[(s + sign * (1 + k)) % N] for k in range(3)]
                arrive += sum(bits(m) for part in engine_plan(topo, T.cores[s], sd) for i, m in part if i == h)
            note("g", [], [land], asem, arrive)
        held.append(("g", call, [src], [land], 0.8, REMOTE))

    both, marks, vals = r("W", 0, WEND), r("W", 0, O + E), r("W", GAP, WEND)
    mdoor, vdoor = r("W", O, O + ND), r("W", TV, TV + ND)
    eye, neg, eyeb, negb, neg2, eyeq, eyea, eyez, eyeg = [r("ID", 128 * i, 128 * i + 128) for i in range(9)]
    zg, zd = r("pq", 128, 128 + ND), r("pcb", 128, 128 + ND)

    def nw(t):
        return NR if t < 2 else NW

    def thr(t, lo, hi):
        return r("QW", QB + 2 * NW * t + lo, QB + 2 * NW * t + hi)

    def block(b, k):
        return r(b, ND * k, ND * k + ND)

    def lists(t, k, m=M):
        return r("P%d" % (t % 3), M * k, M * k + m)

    def offsets(t, k, m=M):
        return r("U%d" % (t & 1), M * k, M * k + m)

    def back(t, m=M):
        return r("Z%d" % (t & 1), 0, m)

    cw = E // XCH
    dma("s", T.kc[:, 192:384], T.k1[:], [], [r("kc", 192, 384)])
    dmas("y", [(T.kr[:, 16 * h:16 * h + 16], T.k0[h:8:2, 2 * ND:2 * ND + 512]) for h in range(2)], [], [r("kr", 0, 32)])
    dma("s", ap(thr(0, 0, NR)), T.q[:], [], [thr(0, 0, NR)])
    for c in range(XCH):
        dmas("y" if c % 2 else "s", [(T.W[:, TV + c * cw:TV + (c + 1) * cw], T.x[:, c * cw:(c + 1) * cw])], [],
             [r("W", TV + c * cw, TV + (c + 1) * cw)], LOCAL + 0.3 * c)
    dma("y", T.kc[:, 0:192], T.k0[:], [], [r("kc", 0, 192)])
    dma("y", T.Xn[:, 0:NR], T.x[:, 2 * ND:2 * ND + NR], [], [r("Xn", 0, NR)])
    iota(r("idf", 0, 128), [[1, 128]], 0, -1)
    op("g", lambda e: e.iota(T.pi[:, 0:1], [[1, 1]], 0, 1), [], [r("pi", 0, 1)])
    iota(r("stf", 0, 288), [[1, 2], [1, 144]], -16, 0)
    iota(r("jraw"), [[16, M]], 0, 1)
    fill(r("W", 0, O), 0)
    fill(r("c85"), int(8.5 * BIG))
    iota(r("wa"), [[16, M]], 0, 0)
    iota(r("wc", 0, 9 * M), [[2 * NW, 9], [0, M]], QB + NW, 0)
    for out, c in ((r("c64"), O), (r("QW", 0, O), 0), (r("QW", O + 2 * ND, O + cw), 0), (r("W", GAP, TV), 0)):
        fill(out, c)
    for t, lo in ((0, 0), (0, NW), (1, 0), (1, NW)):
        fill(thr(t, lo + NR, lo + NW), 100)
    fill(r("c128", 0, NW), -128)

    ts(eye, r("idf", 0, 128), 0.0, None, A.is_equal)
    act(eyeb, eye, F.Silu, scale=B, busy=1500)
    for k, c in enumerate((112, 14, 15)):
        ts(r("pi", 1 + k, 2 + k), r("pi", 0, 1), c, None, A.bitwise_and)
    cp(r("pf", 0, 3), r("pi", 1, 4))
    ms(r("KT", 0, O + E), 0.0)
    ms(r("W", O + ND, O + 768), 0.0)

    def link_table(f):
        lo = 192 * f
        cp(r("kp", 384 + lo, 576 + lo), r("kc", lo, lo + 192))
        tt(r("kp", lo, lo + 192), r("kc", lo, lo + 192), r("kp", 384 + lo, 576 + lo), A.subtract)
        dmas("y", [(T.KT[2 * f + h:128:16, O:O + E], T.kp[:, 384 * h + lo:384 * h + lo + 192]) for h in range(2)],
             [r("kp", lo, lo + 192), r("kp", 384 + lo, 576 + lo)], [r("KT", 0, O + E)])

    link_table(1)
    ts(mdoor, vdoor, 64.0, None, A.add)
    for c in range(1, XCH):
        ts(r("W", O + c * cw, O + (c + 1) * cw), r("W", TV + c * cw, TV + (c + 1) * cw), 64.0, None, A.add)
    ts(r("s3", 0, 32), r("kr", 0, 32), float(O), None, A.add)
    op("v", lambda e: e.transpose(T.aa[:, 0:32], T.s3[:, 0:32]), [r("s3", 0, 32)], [r("aa", 0, 32)])
    cp(r("cu", 0, 24), r("aa", 0, 24))
    act(r("q2", 0, NR), thr(0, 0, NR), F.Identity, bias=62.0)
    act(thr(0, NW, NW + NR), thr(0, 0, NR), F.Identity, bias=63.0)
    ts(thr(0, 0, NR), thr(0, 0, NR), 64.0, None, A.add)
    ts(r("ST", 0, 288), r("stf", 0, 288), T.pf[:, 0:1], -BIG, A.is_equal, A.mult, extra=[r("pf", 0, 1)])
    for lo, hi in ((0, 2 * ND), (cw, 2 * cw), (2 * cw, 3 * cw), (3 * cw, E)):
        act(r("QW", O + lo, O + hi), r("W", TV + lo, TV + hi), F.Identity, bias=62.0)

    def setup_lists():
        ts(r("jj"), r("jraw"), T.pf[:, 0:1], None, A.subtract, extra=[r("pf", 0, 1)])
        ts(r("wb"), r("jraw"), 0.0, T.pf[:, 2:3], A.mult, A.add, extra=[r("pf", 2, 3)])
        ts(r("P0", 0, 24), r("jj", 0, 24), float(2 * ND + O), None, A.add)
        ts(r("P0", 24, M), r("jj", 24, M), float(O - ND), None, A.add)
        for b in (3, 4):
            ts(r("Z0", b * M, b * M + M), r("P0"), float(GAP + 2 * TURN), None, A.add)
        ms(r("P1", 2 * M + 24, 3 * M), 0)
        ts(r("P1", M + 24, 2 * M), r("P0", 24, M), float(GAP), None, A.add)
        for k in range(2):
            ts(r("pf", 4 + k, 5 + k), r("pf", 1, 2), 2.0 * k, -1.0 / BIG, A.is_equal, A.mult)
        ms(r("sg", 24, M), -1.0)
        for m_, c in ((negb, -B), (neg, -1.0), (neg2, -2.0), (eyeq, -NW / B), (eyea, 16 * BIG), (eyez, 2176.0), (eyeg, -GAP / 2)):
            act(m_, eye, F.Copy, scale=c)

    def setup_second():
        link_table(0)
        ms(r("Z1", M, 2 * M), GAP)
        ms(r("P2", 2 * M + 24, 3 * M), 0)
        ts(r("P2", M + 24, 2 * M), r("P0", 24, M), float(GAP), None, A.add)
        cp(r("Z1", 4 * M, 6 * M), r("Z0", 3 * M, 5 * M))

    def setup_third():
        cp(r("Z1", 6 * M, 8 * M), r("Z1", 4 * M, 6 * M))
        cp(r("Z0", 5 * M, 9 * M), r("Z1", 4 * M, 8 * M))
        fill(thr(2, NR, NW), 100)
        iota(r("bdf", 0, 128), [[16, 8], [0, 16]], 0, 0)
        for out, c in ((r("cz", 0, ND), 2176), (r("lv", 0, 64), 0), (r("lw", 0, NW), 0), (r("lw", 1024, 1024 + NW), 0)):
            fill(out, c)
        for k, c in enumerate((256.0, -256.0)):
            ts(r("BD", 128 * k, 128 * k + 128), r("bdf", 0, 128), T.pf[:, 0:1], c, A.is_equal, A.mult, extra=[r("pf", 0, 1)])
        act(r("g0", 0, ND), r("QW", O + ND, O + 2 * ND), F.Identity, bias=-62.0)

    def setup_guests():
        ts(r("s0", 0, 12), r("aa", 24, M), float(O + ND), None, A.is_ge)
        tt(r("s3", 0, 12), r("s0", 0, 12), r("aa", 24, M), A.mult)
        cp(r("gu", 0, 12), r("s3", 0, 12))
        actg(r("gt", 0, ND), r("QW", 0, O + E), r("gu", 0, 12), bias=-63.0)
        tt(r("gb", 0, ND), r("gt", 0, ND), r("g0", 0, ND), A.max)

    def setup_links():
        mm([(r("pk", 128, 512), [(eye, r("kp", 0, 384)), (eye, r("kp", 384, 768))])])
        act(r("kf", 0, 384), r("pk", 128, 512), F.Identity, bias=float(O))
        dmas("y", [(T.L[0:128:16, O + TURN * f:O + TURN * f + E], T.kf[:, 192 * f:192 * f + 192]) for f in range(2)],
             [r("kf", 0, 384)], [r("L", 0, LW)])

    def setup_last():
        for lo in range(0, O + E, 784):
            iota(r("IOT", lo, lo + 784), [[1, 784]], lo - O, 0)
        fill(r("m1", 0, NW), -1)
        ts(r("idf", 0, 128), r("idf", 0, 128), 0.0, None, A.is_equal)
        cp(r("kd", 0, ND), r("kc", 0, ND))
        dmas("y", [(T.yk0[:, 0:ND], T.kd[0:128:16, :]), (T.yk1[:, 0:ND], T.kd[0:128:16, :])], [r("kd", 0, ND)], [])

    def named(t):
        cp(r("cu", 0, nw(t) // 16), r("pk", 0, nw(t) // 16))
        act(r("aa", 0, nw(t) // 16), r("pk", 0, nw(t) // 16), F.Copy)

    def compare(t, lo, hi):
        ttg(r("cmp", lo, hi), marks, r("cu", lo // 16, hi // 16), thr(t, lo, hi), A.is_ge)

    def countw(t):
        wrap("pcnt", "cmp", nw(t), [(eye, r("c85", 0, nw(t) // 16))])

    def before(t):
        f = t & 1
        v, b, st, z = lists(t, 0), back(t), r("st%d" % f), "Z%d" % f
        ts(b, r(z, 3 * M, 4 * M), TURN - 1, None, A.bitwise_and)
        if t > 0:
            if f == 0 or t == 1:
                ts(st, v, float(O + ND), B, A.is_lt, A.mult)
            else:
                ts(r("s0"), v, float(O + ND), B, A.is_lt, A.mult)
                tt(st, r("s0"), r("st0"), A.subtract)
            ts(r("EL%d" % f, 0, 3 * M), r(z, 0, 3 * M), float(-GAP), None, A.add)
            tt(r("s1"), b, st, A.subtract)
            tt(r("bp"), r("s1"), v, A.max)
        for k in (1, 2):
            ts(r(z, k * M, k * M + M), v, float(GAP + TURN * f), None, A.add)
        if t < 9:
            mm([(r("pq"), [(eye, r("wa")), (eye, r("wb")), (eye, r("wc", M * t, M * t + M))]
                 + ([(eyeq, st)] if t > 0 else []))])

    def depth(t):
        return min(t + 1, 9 - t) + 1

    def decide(t):
        m, f = nw(t) // 16, t & 1
        st, k = r("st%d" % f), depth(t)
        tt(r("mm", 0, m), r("aa", 0, m), r("pcnt", 0, m), A.max)
        act(r("sg", 0, m), r("pcnt", 0, m), F.Sign, scale=-1.0)
        tt(lists(t + 1, 1, m), r("mm", 0, m), r("bp", 0, m) if t else back(0, m), A.min)
        if t < 9:
            tt(lists(t + 1, 2, m), r("mm", 0, m), r("pq", 0, m), A.min)
            ts(lists(t + 1, 0), lists(t + 1, 1), GAP - 1, None, A.bitwise_and)
            cp(offsets(t + 1, 0, 3 * M), lists(t + 1, 0, 3 * M))
        else:
            cp(offsets(t + 1, 1), lists(t + 1, 1))
        mm([(r("pm", M * j, M * j + M), [(eyeb, r("sg"))]) for j in range(k)]
           + [(r("pm", 256 + M * j, 256 + M * j + M), [(eye, st)]) for j in range(k) if t > 0]
           + [(r("pm", 512 + M * j, 512 + M * j + M), [(negb, r("sg"))] + ([(neg2, st)] if t > 0 else [])) for j in range(k)])

    def thresholds(t):
        n = nw(t)
        ttg(thr(t + 1, 0, n), r("QW", 0, QB + 2 * NW * (t + 1)), offsets(t + 1, 2, n // 16), r("q2", 0, n), A.max)

    def lowered(t):
        n = nw(t)
        act(r("q2", 0, n), thr(t, 0, n), F.Identity, bias=-2.0)
        act(thr(t, NW, NW + n), thr(t, 0, n), F.Identity, bias=-1.0)

    def kgather(t):
        f, n = t & 1, nw(t)
        vu = offsets(t, 0, n // 16)
        op("s", lambda e: e.activation(T.Kg[:, 0:n], ind(r("KT", 0, O + E), vu), F.Copy, scale=T.pf[:, 4 + f:5 + f]),
           [r("KT", 0, O + E), vu, r("pf", 4, 6)], [r("Kg", 0, n)], 65 + GATHER * n)
        wrap("pk", "Kg", n, [(eye, r("c64", 0, n // 16))])

    def scatter(t, a, b=None):
        u = offsets(t + 1, 1, nw(t) // 16)
        if b is None:
            op("v", lambda e: e.tensor_copy(ind(both, u), ap(a)), [u, a], [both], 50 + SCATTER * nw(t))
        else:
            op("v", lambda e: e.tensor_tensor(ind(both, u), ap(a), ap(b), A.add), [u, a, b], [both], 50 + SCATTER * nw(t))

    def here(t):
        h, u = nw(t) // (1 + (t & 1)), offsets(t, 0)
        for lo in range(0, nw(t), h):
            actg(r("G", lo, lo + h), vals, r(u[0], lo // 16, (lo + h) // 16), bias=-1.0)

    def behind(t, bias=0.0):
        actg(r("Ee", 0, nw(t)), vals, r("EL%d" % (t & 1), 0, nw(t) // 16), bias=bias)

    def differ(n, a, b, early):
        h = n // 2
        for lo, p0 in ((0, 0), (h, 512)):
            out = r("pe", p0, p0 + h)
            terms = [(eye, r(a, lo, lo + h)), (neg, r(b, lo, lo + h))]
            if early == b:
                terms.reverse()
            for k, (x, y) in enumerate(terms):
                op("p", lambda e, x=x, y=y, k=k, out=out: e.matmul(ap(out), ap(x), ap(y), k == 0, k == 1),
                   [x, y] + [out] * k, [out], PE * h)

    def from_differ(out, n, func, **kw):
        for lo, p0 in ((0, 0), (n // 2, 512)):
            act(r(out, lo, lo + n // 2), r("pe", p0, p0 + n // 2), func, **kw)

    def countb(t):
        m = nw(t) // 16
        wrap("pcb", "cmpb", nw(t), [(eye, r("c85", 0, m)), (eye, r("c85", 0, m)), (eyea, r("sg", 0, m))])

    def stack(t):
        f = t & 1
        zo, zn, zw = "Z%d" % f, "Z%d" % (1 - f), M * depth(t)
        tt(r("zm", 0, zw), r(zo, 3 * M, 3 * M + zw), r("pm", 512, 512 + zw), A.min)
        tt(r("pm", 0, zw), r(zo, M, M + zw), r("pm", 0, zw), A.min)
        if t > 0:
            tt(r("zb", 0, zw), r(zo, 2 * M, 2 * M + zw), r("pm", 256, 256 + zw), A.min)
            tt(r("pm", 0, zw), r("zm", 0, zw), r("pm", 0, zw), A.max)
            tt(r(zn, 2 * M, 2 * M + zw), r("zb", 0, zw), r("pm", 0, zw), A.max)
        else:
            tt(r(zn, 2 * M, 2 * M + zw), r("zm", 0, zw), r("pm", 0, zw), A.max)

    def link_values(t):
        f, m = t & 1, nw(t) // 16
        if t == 0:
            cp(r("lv", 0, m), back(0, m))
        else:
            tt(r("s2", 0, m), lists(t, 0, m), r("pcb", 0, m), A.max)
            tt(r("lv", 0, m), r("s2", 0, m), back(t, m), A.min)
        nb = (m + 31) // 32
        lt = r("lt", 64 * f, 64 * f + 32 * nb)
        op("v", lambda e: e.transpose(ap(lt), T.lv[:, 0:32 * nb]), [r("lv", 0, 64)], [lt])
        dmas("y", [(T.lw[16 * h:128:32, 1024 * f + 512 * b:1024 * f + 512 * b + 512],
                    T.lt[:, 64 * f + 32 * b + 16 * h:64 * f + 32 * b + 16 * h + 16]) for b in range(nb) for h in range(2)],
             [lt], [r("lw", 1024 * f, 1024 * f + 1024)])

    def last_values(t):
        tt(r("s2"), lists(t, 0), r("pcb"), A.max)
        tt(r("li"), r("s2"), back(t), A.min)
        ts(r("li"), r("li"), GAP - 1, None, A.bitwise_and)
        cp(r("lu"), r("li"))
        actg(r("lx", NW * (t & 1), NW * (t & 1) + NW), r("IOT", 0, O + E), r("lu"))

    def link_write(t):
        n = nw(t)
        lo = r("EL%d" % (1 - (t & 1)), 2 * M, 2 * M + n // 16)
        if t < 8:
            lw = r("lw", 1024 * (t & 1), 1024 * (t & 1) + n)
            op("s", lambda e: e.activation(ind(r("L", 0, LW), lo), ap(lw), F.Silu), [lo, lw], [r("L", 0, LW)], 65 + SCATTER * n)
        else:
            lw = r("lx", NW * (t & 1), NW * (t & 1) + NW)
            op("v", lambda e: e.tensor_copy(ind(r("L", 0, LW), lo), ap(lw)), [lo, lw], [r("L", 0, LW)], 50 + SCATTER * n)

    def link_rows(f):
        return T.L[0:128:16, O + TURN * f + ND:O + TURN * f + E]

    def round_links():
        cc, cs, ps = r("cc", 0, 2 * CW), r("cs", 0, 2 * CW), r("pk", 128, 128 + 2 * CW)
        dmas("y", [(T.cc[:, CW * f:CW * f + CW], link_rows(f)) for f in range(2)], [r("L", 0, LW)], [cc])
        act(cs, cc, F.Sign, bias=-4000.0)
        mm([(ps, [(r("idf", 0, 128), cc), (eyeg, cs)])])
        act(cc, ps, F.Identity, bias=MAGIC)
        act(cc, cc, F.Identity, bias=-MAGIC - GAP // 2 - O)
        dmas("y", [(link_rows(f), T.cc[:, CW * f:CW * f + CW]) for f in range(2)], [cc], [r("L", 0, LW)])

    def guests_back(ph):
        mm([(zg, [(eyez, r("se", 0, ND)), (r("BD", 128, 256), r("cmp", NR, NW))])])
        tt(r("u2", 0, ND), r("gb", 0, ND), zg, A.min)
        tt(block("snd", ph - 1), r("u2", 0, ND), r("g0", 0, ND), A.max)
        exchange(-1, block("snd", ph - 1), block("rb", ph - 1), "ba%d" % (ph - 1), "bl%d" % (ph - 1))

    def doors_take(ph):
        tt(r("t1", 0, ND), block("rb", ph - 1), block("mk", (ph - 1) & 1), A.min)
        tt(vdoor, r("vd", 0, ND), r("t1", 0, ND), A.max)

    def doors_clear(ph):
        mm([(zd, [(eye, vdoor), (neg, block("mk", ph & 1))])])
        act(r("vd", 0, ND), zd, F.Relu)

    compare(0, 0, NR)
    countw(0)
    setup_lists()
    before(0)
    for ph in range(5):
        t = 2 * ph
        n = nw(t)
        decide(t)
        scatter(t, r("Xn", 0, n))
        kgather(t + 1)
        thresholds(t)
        t += 1
        named(t)
        if ph > 0:
            act(r("se", 0, ND), zg, F.Sign)
            compare(t, NR, NW)
            guests_back(ph)
        compare(t, 0, NR)
        countw(t)
        if ph == 0:
            setup_second()
        stack(t - 1)
        if ph > 0:
            link_write(t - 3)
        before(t)
        if ph > 0:
            from_differ("cmpb", n, F.Sign, bias=1.5, scale=-1.0)
            countb(t - 1)
            doors_clear(ph - 1)
        if ph == 4:
            break
        lowered(t)
        behind(t)
        decide(t)
        thresholds(t)
        scatter(t, thr(t + 1, 0, n), r("c128", 0, n))
        act(block("rp", ph), mdoor, F.Identity, bias=128.0)
        exchange(1, block("rp", ph), block("rf", ph), "fa%d" % ph, "fl%d" % ph)
        if ph > 0:
            doors_take(ph)
        here(t)
        differ(n, "G", "Ee", "Ee")
        from_differ("Rv", n, F.Relu)
        scatter(t, r("Ee", 0, n), r("Rv", 0, n))
        from_differ("cmpb", n, F.Sign, bias=1.5)
        kgather(t + 1)
        if ph == 0:
            setup_third()
        stack(t)
        if ph > 0:
            link_write(t - 2)
        link_values(t - 1)
        t += 1
        before(t)
        here(t)
        named(t)
        compare(t, 0, NR)
        tt(thr(t, NR, NW), thr(t, NR, NW), block("rf", ph), A.min)
        compare(t, NR, NW)
        countw(t)
        ttg(r("Xn", 0, NW), vals, r("EL0"), r("G", 0, NW), A.max)
        differ(NW, "Xn", "G", "G")
        lowered(t)
        mm([(zg, [(neg, r("cz", 0, ND)), (r("BD", 0, 128), r("cmp", NR, NW))])])
        act(block("mk", ph & 1), block("rp", ph), F.Relu, bias=108.0, scale=-1.0)
        countb(t - 1)
        link_values(t - 1)
        if ph == 0:
            setup_guests()
            setup_links()
        if ph == 2:
            setup_last()

    behind(9, 1.0)
    last_values(8)
    decide(9)
    link_write(7)
    round_links()
    doors_take(4)
    ttg(r("Xn", 0, NW), vals, offsets(9, 0), r("Ee", 0, NW), A.max)
    here(9)
    scatter(9, r("Xn", 0, NW), r("m1", 0, NW))
    for c in range(2):
        dmas("y" if c else "s", [(T.yx[:, 1536 * c:1536 * c + 1536], T.W[:, TV + 1536 * c:TV + 1536 * c + 1536])], [vals], [], 5.5)
    differ(NW, "G", "Ee", "Ee")
    from_differ("cmpb", NW, F.Sign, bias=2.5)
    countb(9)
    last_values(9)
    link_write(8)
    stack(9)
    ts(r("EL0", 2 * M, 3 * M), r("Z0", 2 * M, 3 * M), float(-GAP), None, A.add)
    link_write(9)
    dma("y", T.yk0[:, ND:E], link_rows(0), [r("L", 0, LW)], [])
    dma("s", T.yk1[:, ND:E], link_rows(1), [r("L", 0, LW)], [])

    if not TURNS:
        TURNS.extend(plan_turns(held))
    for k in TURNS:
        held[k][1]()
    for sem in total:
        wait("y", sem, total[sem])
